import numpy as np, ml_dtypes
CORES = [2,3,42,43,82,83,122,123]
N = 8
BF = ml_dtypes.bfloat16
def gentries(a):
    return np.ascontiguousarray(a.reshape(8, 16, -1).transpose(0, 2, 1)).reshape(8, -1)
def gtable(e):
    e = np.asarray(e); return np.ascontiguousarray(e.reshape(8, -1, 16).transpose(0, 2, 1)).reshape(128, -1).astype(np.int32)
W, NW, P, RO, F = 4096, 512, 8, 3, 1
S = W // NW
def parts(rng):
    x = rng.integers(0, 16, (N, 8, 16, W)); l = rng.integers(0, W, (N, 8, NW, P))
    n = np.where(rng.random((N, 8, NW)) < 0.12, rng.integers(0, P + 1, (N, 8, NW)), rng.integers(P // 2, P + 1, (N, 8, NW)))
    return x, l, n, rng.integers(0, 256, (N, 8, 16)), rng.integers(68, 100, (N, 8))
def pack(x, l, n, w, t):
    return {"xv": np.ascontiguousarray(x.reshape(N, 128, W)).astype(np.float32).astype(BF), "wl": np.stack([gtable(a.reshape(8, NW * P)) for a in l]),
            "wn": np.ascontiguousarray(n).astype(np.int32), "wt": np.ascontiguousarray(w.reshape(N, 128, 1)).astype(np.int32), "th": np.ascontiguousarray(t.reshape(N, 8, 1)).astype(np.int32)}
def setup_inputs(rng):
    return pack(*parts(rng))
def setup_inputs_alike(rng):
    x, l, n, w, t = parts(rng)
    l[:, ::2] = rng.choice(np.array([0, W - 1, W // 2, 3]), (N, 4, NW, P))
    l[:, 1] = l[:, 1, :, :1]; x[:, 3] = x[:, 3, :, :1]; w[:, 5] = 0; n[:, 6] = P; t[:, 7] = 0
    return pack(x, l, n, w, t)
def setup_inputs_corners(rng):
    x, l, n, w, t = parts(rng); k = np.arange(P)
    x = rng.integers(0, 4, (N, 8, 16, W)) + 12 * (np.arange(W) & 1); t = rng.integers(48, 144, (N, 8)); t[:, 0] = 48; t[:, 7] = 143
    w = np.where(rng.random((N, 8, 1)) < 0.3, 255 * rng.integers(0, 2, (N, 8, 1)), w)
    n = rng.choice(np.array([0, 1, 2, P - 1, P, P, P, P]), (N, 8, NW)); m = np.minimum(n, rng.choice(np.array([1, 2, P // 2, P // 2 + 1, P - 1, P]), (N, 8, NW)))
    pick = rng.random((8, NW)) < 0.4; a = rng.integers(P // 2, P + 1, (8, NW)); a[:, 0] = P // 2 + 1; a[:, NW - 1] = P; pick[:, 0] = True; pick[:, NW - 1] = True
    for q in range(0, N - 1, 2):
        m[q] = np.where(pick, a, m[q]); n[q] = np.where(pick, np.maximum(a, rng.integers(0, P + 1, (8, NW))), n[q])
        m[q + 1] = np.where(pick, P - a, m[q + 1]); n[q + 1] = np.where(pick, np.where(a == P, 0, np.maximum(P - a, rng.integers(1, P + 1, (8, NW)))), n[q + 1])
    m[0, 5] = P; n[0, 5] = P; m[1, 4] = 0; n[1, 4] = 0
    m[N - 2] = P; n[N - 2] = P; m[N - 1] = 0; n[N - 1] = 0
    for q in (0, 1):
        fr = np.where(pick, 0, m[q]); fr[5] = 0; fr = fr.reshape(-1); o = rng.permutation(8 * NW); b = fr[o]; cut = np.zeros_like(b)
        cut[o] = np.clip((int(np.sum(m[q])) - 256) % 512 - (np.add.accumulate(b) - b), 0, b)
        m[q] = m[q] - cut.reshape(8, NW); n[q] = np.where(m[q] == 0, 0, n[q])
    sc = np.where((k == 0) | (k >= n[..., None]), 2.0, rng.random((N, 8, NW, P)))
    brk = np.argsort(np.argsort(sc, axis=-1), axis=-1) < (m - 1)[..., None]
    cl = (rng.integers(0, 2, (N, 8, NW, 1)) + np.add.accumulate(brk.astype(np.int64), axis=-1)) & 1
    l = np.where(rng.random((N, 8, NW, P)) < 0.1, cl * (W - 1), 2 * rng.integers(0, W // 2, (N, 8, NW, P)) + cl)
    return pack(x, l, n, w, t)
def setup_inputs_ends(rng):
    kind = rng.integers(0, 3, (N, 8, 1, W)); k = np.arange(P); c = np.arange(1, P + 1)
    x = np.where(kind == 0, 0, np.where(kind == 1, 15, 15 * rng.integers(0, 2, (N, 8, 16, W))))
    for u, v in ((0, 15), ((240 * 255) & (W - 1), 0)):
        hh = ((u * u >> 5) + 37 * u + 611 * c) & (W - 1)
        for g in (0, 7): x[:, g][..., hh] = v
    x[..., 0] = 0; x[..., W - 1] = 15
    w = 255 * rng.integers(0, 2, (N, 8, 16)); w[:, 0] = 255; w[:, 7] = 255; w[:, 3, 0] = 0; w[:, 4] = 0
    t = 239 * rng.integers(0, 2, (N, 8)); t[:, 0] = 0; t[:, 1] = 239; t[:, 7] = 239
    kd = rng.integers(0, 4, (N, 8, NW, 1)); s = rng.integers(0, 2, (N, 8, NW, 1)); em = np.where(np.arange(N) == N - 1, 0.05, 0.25).reshape(N, 1, 1)
    kd[N - 1] = np.where(rng.random((8, NW, 1)) < 0.9, 1, kd[N - 1]); kd[:, :, 0] = 1; kd[:, 7, NW - 1] = 1; kd[:, 7, NW - 2] = 0; s[:, 7, NW - 2] = 1
    b = np.where(kd == 0, s, np.where(kd == 1, (k + s) & 1, rng.integers(0, 2, (N, 8, NW, P))))
    n = P * (rng.random((N, 8, NW)) > em).astype(np.int64); n[:, :, 0] = P; n[:, :, 1] = 0; n[:, :, NW - 2] = P; n[:, :, NW - 1] = P
    return pack(x, (W - 1) * b, n, w, t)
def setup_inputs_spread(rng):
    x, l, n, w, t = parts(rng)
    x = (rng.random((N, 8, 16, W)) * np.exp2(rng.integers(0, 5, (N, 8, 1, W)))).astype(np.int64)
    l = np.minimum((W * rng.random((N, 8, NW, P)) ** rng.choice(np.array([0.3, 1.0, 3.0]), (N, 8, 1, 1))).astype(np.int64), W - 1)
    n = rng.integers(0, P + 1, (N, 8, NW)); w = (256 * rng.random((N, 8, 16)) ** 2).astype(np.int64)
    t = np.exp2(7.9 * rng.random((N, 8))).astype(np.int64) - 1
    return pack(x, l, n, w, t)
def setup_inputs_ties(rng):
    x, l, n, w, t = parts(rng)
    lane = np.argsort(rng.random((N, 8, 16)), axis=-1); pm = np.argsort(rng.random((N, 8, W)), axis=-1)
    lev = np.zeros((N, 8, W), np.int64); np.put_along_axis(lev, pm, np.broadcast_to(np.arange(W) % 241, (N, 8, W)), 2)
    x = np.clip(lev[:, :, None, :] - 15 * lane[..., None], 0, 15)
    t = rng.choice(np.array([0, 1, 15, 16, 47, 80, 100]), (N, 8)); s = rng.integers(0, 241, (N, 8, NW))
    for k in range(P):
        l[..., k] = np.take_along_axis(pm, s + 241 * rng.integers(0, W // 241, (N, 8, NW)), 2)
        st = np.abs(t[:, :, None] + rng.integers(-1, 2, (N, 8, NW))); up = ((rng.random((N, 8, NW)) < 0.5) & (s + st <= 240)) | (s - st < 0)
        s = np.where(up, s + st, s - st)
    t[:, 7] = 239
    hl = 239 * ((np.arange(P) + rng.integers(0, 2, (N, NW, 1))) & 1) + rng.integers(0, 2, (N, NW, P)) + 241 * rng.integers(0, W // 241, (N, NW, P))
    l[:, 7] = np.take_along_axis(pm[:, 7], hl.reshape(N, NW * P), 1).reshape(N, NW, P)
    return pack(x, l, n, w, t)
def check_inputs(d):
    bad = []
    for k, lo, hi in (("xv", 0, 15), ("wl", 0, W - 1), ("wn", 0, P), ("wt", 0, 255), ("th", 0, 239)):
        v = np.asarray(d[k]).astype(np.float64)
        if not (np.min(v) >= lo and np.max(v) <= hi): bad.append("range of " + k)
        elif np.any(v != np.floor(v)): bad.append("whole numbers of " + k)
    return bad
def reference(xv, wl, wn, wt, th):
    x = xv.astype(np.int32).reshape(N, 8, 16, W); w = wt.astype(np.int32).reshape(N, 8, 16, 1, 1); lim = th.astype(np.int64).reshape(N, 8, 1, 1)
    l = np.stack([gentries(a) for a in wl]).astype(np.int64).reshape(N, 8, NW, P); n = wn.astype(np.int64)
    last = np.zeros((N, 1, 1, 1), np.int64); k = np.arange(P); M = W - 1
    for t in range(RO):
        if t > 0:
            l = np.roll(l, (1, 1), axis=(0, 1)); n = np.roll(n, (1, 1), axis=(0, 1))
        live = k < n[..., None]
        v = np.take_along_axis(x, l.reshape(N, 8, 1, NW * P), 3).reshape(N, 8, 16, NW, P)
        dist = np.add.reduce(np.abs(v[..., 1:] - v[..., :-1]), axis=2)
        start = live.copy(); start[..., 1:] &= dist > lim
        end = live.copy(); end[..., :-1] &= start[..., 1:] | ~live[..., 1:]
        num = np.add.accumulate(start.astype(np.int64), axis=-1) - 1; m = np.add.reduce(start.astype(np.int64), axis=-1)
        z = v.copy(); c = np.ones((N, 8, NW, P), np.int64); f = l.copy()
        for j in range(1, P):
            s = start[..., j]
            z[..., j] = np.where(s[:, :, None], v[..., j], np.maximum(z[..., j - 1], v[..., j]))
            c[..., j] = np.where(s, 1, c[..., j - 1] + 1); f[..., j] = np.where(s, l[..., j], f[..., j - 1])
        u = np.add.reduce(w * z, axis=2).astype(np.int64) & M
        h = ((u * u >> 5) + 37 * u + 611 * c) & M
        xh = np.take_along_axis(x, h.reshape(N, 8, 1, NW * P), 3).reshape(N, 8, 16, NW, P)
        dd = np.add.reduce(np.abs(xh - z), axis=2).astype(np.int64)
        y = np.zeros((N, 8, NW, 2 * P + 2), np.int64)
        np.put_along_axis(y, np.where(end, 2 * num, 2 * P), ((f * (2 * c + 1) >> 2) + last) & M, 3)
        np.put_along_axis(y, np.where(end, 2 * num + 1, 2 * P + 1), (h + dd * (2 * c + 1)) & M, 3)
        own = np.minimum(2 * m, P); over = np.roll(2 * m - own, 1, axis=0); oy = np.roll(y[..., P:2 * P], 1, axis=0)
        n = np.minimum(own + over, P); o = own[..., None]
        l = np.where(k < o, y[..., :P], np.where(k < n[..., None], np.take_along_axis(oy, np.clip(k - o, 0, P - 1), 3), 0))
        e = np.argmax(end, axis=-1)[..., None]; e5 = e[:, :, None]
        val = ((np.take_along_axis(z, e5, 4) + np.take_along_axis(xh, e5, 4)) >> 1)[..., 0]
        at = (S * np.arange(NW) + (np.take_along_axis(u, e, 3)[..., 0] & (S - 1)))[:, :, None]
        np.put_along_axis(x, at, np.where((m > 0)[:, :, None], val, np.take_along_axis(x, at, 3)), 3)
        last = np.add.reduce(m.reshape(N, 8 * NW), axis=1).reshape(N, 1, 1, 1) & 255
    return {"yx": np.add.reduce(x.reshape(N, 128, W // F, F), axis=3).astype(np.float32).astype(BF), "yl": np.stack([gtable(a.reshape(8, NW * P)) for a in l]).astype(np.float32), "yn": n.astype(np.float32)}

@@ -1,0 +1,548 @@
+from concourse.bass import DstId, RemoteDMATransfer
+from concourse.mybir import dt, AluOpType, AxisListType, ActivationFunctionType
+
+NV, W = 3, 4096
+GC = 1024
+BFT, F32, I32, U16 = "bfloat16", "float32", "int32", "uint16"
+SCRATCH = {}
+VIEWS = {}
+
+
+def _sb(name, shape, ty):
+    buf = "b_" + "_".join(str(n) for n in shape) + "_" + ty
+    k = SCRATCH[buf][1][1] if buf in SCRATCH else 0
+    SCRATCH[buf] = ("sbuf", [shape[0], k + 1] + shape[1:], ty)
+    VIEWS[name] = (buf, k)
+
+
+SCRATCH["X"] = ("sbuf", [128, 8192], BFT)
+SCRATCH["Z"] = ("sbuf", [128, 4096], BFT)
+for _n in ("L0", "L1", "L2", "PT", "W0", "W1", "UB"):
+    SCRATCH[_n] = ("psum", [128, 512], F32)
+SCRATCH["PV"] = ("psum", [128, 4, 16, 8], F32)
+for _n, _s, _t in (
+        ("ONES", [128, 128], BFT), ("B1", [128, 128], BFT), ("B", [128, 128], BFT), ("IB", [128, 128], BFT), ("NIB", [128, 128], BFT),
+        ("NB", [128, 128], BFT), ("N4", [128, 128], BFT), ("P4", [128, 128], BFT), ("P16", [128, 128], BFT), ("CL", [128, 128], BFT),
+        ("CR", [128, 512], BFT), ("IDF", [128, 128], F32), ("PR32", [128, 32], F32), ("E81", [8, 128], BFT), ("E8", [8, 128], BFT),
+        ("BIASC", [128, 16, 8], BFT), ("WM", [128, 8], BFT), ("KA0", [128, 16, 8], BFT), ("KA1", [128, 16, 8], BFT), ("KB", [128, 16, 8], BFT),
+        ("NK0", [128, 128], BFT), ("C129", [128, 16, 8], BFT), ("C128", [128, 16, 8], BFT),
+        ("FR", [128, 256], F32), ("CRO", [128, 512], F32), ("CRV", [128, 256], F32), ("THB", [8, 1], BFT), ("THF", [8, 1], F32), ("DT", [8, 8], BFT),
+        ("PID", [128, 1], I32), ("PI2", [128, 1], I32), ("WT", [128, 4], I32), ("AI", [128, 1], I32), ("AI2", [128, 1], I32), ("BX", [128, 1], I32), ("BY", [128, 1], I32),
+        ("NZ", [128, 1], F32), ("COEF", [128, 1], F32), ("WCOL", [128, 1], F32), ("AR", [128, 1], F32), ("A4", [128, 1], F32), ("CSQ", [128, 1], F32), ("CCT", [128, 1], F32),
+        ("K1", [128, 1], F32), ("K2", [128, 1], F32), ("KM", [128, 1], F32), ("KZ", [128, 1], F32), ("PF0", [128, 1], F32), ("PF1", [128, 1], F32), ("BA", [128, 1], F32), ("BB", [128, 1], F32), ("BC", [128, 1], F32),
+        ("BD", [128, 1], F32), ("BE", [128, 1], F32), ("TH", [8, 1], I32), ("WN", [8, 512], I32), ("WNF", [8, 512], F32), ("WL", [128, 256], I32),
+        ("BW1", [128, 32], I32), ("BW0", [128, 32], I32), ("L7", [128, 32], I32), ("FVM", [128, 256], F32), ("LI", [128, 64], I32), ("LQ", [128, 96], I32),
+        ("LOFF", [128, 96], U16), ("ZS", [128, 512], F32), ("ZX", [128, 512], BFT), ("ZI", [128, 512], BFT), ("YN", [8, 512], F32)):
+    _sb(_n, _s, _t)
+for _b in "01":
+    for _n, _s, _t in (
+            ("V", [128, 2064], BFT), ("AD", [128, 2048], BFT), ("XH", [128, 2048], BFT), ("AE", [128, 2048], BFT),
+            ("OFF", [128, 128], U16), ("HOFF", [128, 128], U16), ("DEAD", [128, 16, 8], BFT), ("NM", [128, 16, 8], I32), ("NF", [128, 128], F32),
+            ("S", [128, 16, 9], BFT), ("NS", [128, 128], BFT), ("SP", [128, 128], BFT), ("C", [128, 128], BFT), ("CN", [128, 128], BFT), ("CE", [128, 16, 8], BFT),
+            ("CX", [128, 16, 4], BFT), ("SN", [128, 128], F32), ("AX", [128, 128], F32), ("T0", [128, 16, 8], F32), ("TI", [128, 16, 8], I32), ("TJ", [128, 16, 8], I32),
+            ("KP", [128, 16, 8], BFT), ("CT", [128, 16, 8], F32), ("WI", [128, 16, 8], I32), ("HI", [128, 16, 8], I32), ("HF", [128, 128], F32),
+            ("FS", [128, 256], F32), ("FO", [128, 256], F32),
+            ("MO", [128, 512], BFT), ("MV", [128, 256], BFT), ("N2", [128, 16, 8], I32), ("N3", [128, 16, 8], I32),
+            ("PRO", [128, 512], F32), ("PRV", [128, 256], F32), ("OSO", [128, 512], F32), ("OSV", [128, 256], F32),
+            ("J", [128, 16, 4], I32), ("JM", [128, 16, 4], I32), ("YL", [128, 128], F32), ("NA", [128, 16, 4], F32), ("NC", [128, 16, 2], F32), ("NN", [128, 16], F32)):
+        _sb(_n + _b, _s, _t)
+    for _i in range(NV):
+        for _n in ("SO", "SV", "RO", "RV"):
+            _sb("%s%d%s" % (_n, _i, _b), [128, 16, 4], F32)
+        for _n in ("MX", "MR"):
+            _sb("%s%d%s" % (_n, _i, _b), [128, 16], BFT)
+
+DMAS = ["xv", "wl", "wn", "wt", "th", "yx", "yl0", "yl1", "yn"]
+SEMAPHORES = ["qv", "qs", "qp", "qg", "ls"] + ["d_" + n for n in DMAS] + ["r%s%d%d" % (k, t, b) for k in "xm" for t in range(NV) for b in (0, 1)]
+CY = 0.00104
+PC = 0.00052
+HOP = 0.08
+
+
+def rank_program(g, core, T, topo):
+    rank = T.rank_of(core)
+    if rank is None:
+        return
+    n = len(T.cores)
+    nxt, nx2, prv, pr2 = [T.cores[(rank + k) % n] for k in (1, 2, -1, -2)]
+    A, F = AluOpType, ActivationFunctionType
+    V, S, P = g.vector, g.scalar, g.tensor
+    D = {k: T[b][:, i] for k, (b, i) in VIEWS.items()}
+    X, Z, PT, PV, L = T.X, T.Z, T.PT, T.PV, [T.L0, T.L1, T.L2]
+    tiles = [slice(128 * k, 128 * k + 128) for k in range(4)]
+    UB, WB = [T.UB[:, k] for k in tiles], [[w[:, k] for k in tiles] for w in (T.W0, T.W1)]
+    tt, mm, sc, act, mset, copy = V.tensor_tensor, P.matmul, V.tensor_tensor_scan, S.activation, V.memset, V.tensor_copy
+    ops, cur = [], [""]
+
+    def op(q, r, w, cost, fn, b=(), sem=None, inc=0, after=(), lat=0.0):
+        ops.append({"k": cur[0] + q if cur[0] else "", "q": q, "r": r.split(), "w": w.split(), "cost": cost, "fn": fn, "b": list(b), "sem": sem, "inc": inc, "after": list(after), "lat": lat})
+        return len(ops) - 1
+
+    def v(r, w, cyc, fn, b=()):
+        return op("v", r, w, 0.03 + CY * max(cyc, 64), lambda: [fn()], b)
+
+    def s(r, w, cyc, fn, b=()):
+        return op("s", r, w, 0.03 + CY * max(cyc, 64), lambda: [fn()], b)
+
+    def p(r, w, cyc, fn, b):
+        return op("p", r, w, PC * cyc, fn, b)
+
+    def gg(r, w, cost, fn):
+        return op("g", r, w, cost, lambda: [fn()])
+
+    def ld(q, name, out, in_, r, w, cost):
+        return op(q, r, w, 0.06, lambda: [(g.sync if q == "y" else S).dma_start(out, in_)], sem="d_" + name, inc=16, lat=cost)
+
+    def ts(out, in0, s1, s2, o0, o1=None):
+        if o1 is None:
+            return V.tensor_scalar(out, in0, s1, None, o0)
+        return V.tensor_scalar(out, in0, s1, s2, o0, o1)
+
+    def gcopy(out, in_, n):
+        return g.affine_select(out, in_, [[0, n]], A.is_equal, 0.0, 0, 0)
+
+    nl = [0]
+
+    def lane():
+        nl[0] += 1
+        return (nl[0] - 1) % len(L)
+
+    ld("y", "wl", D["WL"], T.wl[:], "", "WL", 2.0)
+    ld("y", "xv", X[:, 0:W], T.xv[:], "", "X", 7.0)
+    ld("d", "th", D["TH"], T.th[:], "", "TH", 2.0)
+    ld("d", "wt", D["WT"][:, 0:1], T.wt[:], "", "WT", 2.0)
+    ld("d", "wn", D["WN"], T.wn[:], "", "WN", 2.0)
+    v("", "ONES", 64, lambda: mset(D["ONES"], 1.0))
+    gg("ONES", "B1", 0.5, lambda: g.affine_select(D["B1"], D["ONES"], [[-16, 8], [0, 16]], A.is_ge, 0.0, 0, 1))
+    gg("B1", "B", 0.5, lambda: g.affine_select(D["B"], D["B1"], [[16, 8], [0, 16]], A.is_ge, 0.0, 15, -1))
+    gg("ONES", "IB", 0.5, lambda: g.affine_select(D["IB"], D["ONES"], [[-1, 128]], A.is_equal, 0.0, 0, 1))
+    gg("ONES", "E81", 0.5, lambda: g.affine_select(D["E81"], T.b_128_128_bfloat16[0:8, VIEWS["ONES"][1]], [[1, 128]], A.is_ge, 0.0, 0, -16))
+    gg("E81", "E8", 0.5, lambda: g.affine_select(D["E8"], D["E81"], [[-1, 128]], A.is_ge, 0.0, 15, 16))
+    gg("", "PID", 0.2, lambda: g.iota(D["PID"], [[0, 1]], 0, 1))
+    gg("", "BW1", 0.3, lambda: g.iota(D["BW1"], [[16, 32]], 0, 0))
+    for b in (0, 1):
+        v("WL", "OFF%d" % b, 128, lambda b=b: copy(D["OFF%d" % b], D["WL"][:, 128 * b:128 * b + 128]))
+        v("", "V%dz" % b, 64, lambda b=b: mset(D["V%d" % b][:, 0:16], 0.0))
+        v("", "S%d9" % b, 64, lambda b=b: mset(D["S%d" % b][:, :, 8], 1.0))
+    v("IB", "IDF", 128, lambda: copy(D["IDF"], D["IB"]))
+    for k, src, c in (("NIB", "IB", -1.0), ("NB", "B", -16.0), ("N4", "IB", -4096.0), ("P4", "IB", 4096.0), ("P16", "IB", 65536.0)):
+        v(src, k, 64, lambda k=k, src=src, c=c: ts(D[k], D[src], c, None, A.mult))
+    v("", "CRa", 256, lambda: mset(D["CR"], 1.0))
+    v("CRa", "CR", 64, lambda: mset(D["CR"][:, 0:512:8], -64.0))
+    v("TH", "THB", 64, lambda: copy(D["THB"], D["TH"]))
+    v("TH", "THF", 64, lambda: copy(D["THF"], D["TH"]))
+    v("PID", "PI2", 64, lambda: ts(D["PI2"], D["PID"], 15, None, A.bitwise_and))
+    v("PI2", "NZ", 64, lambda: ts(D["NZ"], D["PI2"], 0.0, None, A.is_gt))
+    p("E8 THB", "PTth", 64, lambda: [mm(PT[:, 304:305], D["E8"], D["THB"], True, True)], ["PT"])
+    v("PTth NZ", "COEF", 64, lambda: tt(D["COEF"], PT[:, 304:305], D["NZ"], A.add), ["PT"])
+    v("B COEF", "CL", 64, lambda: ts(D["CL"], D["B"], D["COEF"], None, A.mult))
+    v("THF IB", "DT", 64, lambda: ts(D["DT"], D["IB"][0:8, 0:8], D["THF"], None, A.mult))
+    p("ONES DT", "W0.0", 1024, lambda: [mm(WB[0][0][:, m:128:16], D["ONES"][0:8, :], D["DT"], True, True) for m in range(16)], ["W0"])
+    v("W0.0", "BIa", 128, lambda: ts(D["BIASC"], WB[0][0], -1.0, None, A.mult), ["W0"])
+    v("BIa", "BIASC", 64, lambda: mset(D["BIASC"][:, :, 0], 8192.0))
+    v("WT", "WCOL", 64, lambda: copy(D["WCOL"], D["WT"][:, 0:1]))
+    v("B WCOL", "WM", 64, lambda: ts(D["WM"], D["B"][:, 0:128:16], D["WCOL"], None, A.mult))
+    for k, c in (("C129", 129.0), ("C128", 128.0), ("A4", 0.0), ("CSQ", 4096.0 + 592.0), ("CCT", -360240.0), ("K1", 1.0), ("K2", 2.0), ("KM", -1.0), ("KZ", 257.5)):
+        v("", k, 64, lambda k=k, c=c: mset(D[k], c))
+    v("", "NKa", 64, lambda: mset(D["NK0"], 1.0))
+    v("NKa", "NK0", 64, lambda: mset(D["NK0"][:, 0::8], 0.0))
+    v("WN", "WNF", 512, lambda: copy(D["WNF"], D["WN"]))
+    for b in (0, 1):
+        p("WNF IDF", "PTn%d" % b, 512, lambda b=b: [P.transpose(PT[:, 320 + 16 * b + w1:336 + 16 * b:2], D["WNF"][:, 256 * b + w1:256 * b + 256:2], D["IDF"][0:8, 0:8]) for w1 in (0, 1)], ["PT"])
+        for k in range(8):
+            v("PTn%d" % b + (" " + " ".join("DE%d%d" % (b, i) for i in range(7)) if k == 7 else ""), "DEAD%d" % b if k == 7 else "DE%d%d" % (b, k), 64,
+              lambda b=b, k=k: ts(D["DEAD%d" % b][:, :, k], PT[:, 320 + 16 * b:336 + 16 * b], float(k), None, A.is_le), ["PT"])
+        v("WL", "NF%d" % b, 128, lambda b=b: copy(D["NF%d" % b], D["WL"][:, 128 * b:128 * b + 128]))
+        p("NF%d IDF" % b, "PTN", 512, lambda b=b: [P.transpose(PT[:, 128:256], D["NF%d" % b], D["IDF"])], ["PT"])
+        v("PTN", "NM%d" % b, 128, lambda b=b: copy(D["NM%d" % b], PT[:, 128:256]), ["PT"])
+
+    def late_constants():
+        v("", "FRa", 256, lambda: mset(D["FR"], 1.0))
+        v("FRa", "FR", 64, lambda: mset(D["FR"][:, 0::8], 0.0))
+        v("", "CROa", 512, lambda: mset(D["CRO"], 1.0))
+        v("CROa", "CRO", 64, lambda: mset(D["CRO"][:, 0::8], 0.0))
+        v("", "CRVa", 256, lambda: mset(D["CRV"], 1.0))
+        v("CRVa", "CRV", 64, lambda: mset(D["CRV"][:, 0::4], 0.0))
+        v("", "FVM", 256, lambda: mset(D["FVM"], 0.0))
+        v("PID", "PF0", 64, lambda: copy(D["PF0"], D["PID"]))
+        v("PF0", "PF1", 64, lambda: ts(D["PF1"], D["PF0"], 128.0, None, A.add))
+        for b in (0, 1):
+            v("PF%d C129" % b, "KA%d" % b, 64, lambda b=b: ts(D["KA%d" % b], D["C129"], 0.0, D["PF%d" % b], A.mult, A.add))
+        for k in range(16):
+            v("", "KB.%d" % k, 64, lambda k=k: mset(D["KB"][:, k // 8::2, k % 8], float(k)))
+        for q in range(4):
+            v("IDF", "PR%d" % q, 64, lambda q=q: copy(D["PR32"][32 * q:32 * q + 32, :], D["IDF"][32 * q:32 * q + 32, 32 * q:32 * q + 32]))
+        v("PI2", "BX", 64, lambda: ts(D["BX"], D["PI2"], 3, None, A.bitwise_and))
+        v("PI2", "BY", 64, lambda: ts(D["BY"], D["PI2"], 2, 1, A.arith_shift_right, A.bitwise_and))
+        v("BX", "BA", 64, lambda: ts(D["BA"], D["BX"], 512.0, None, A.mult))
+        v("BY", "BB", 64, lambda: ts(D["BB"], D["BY"], 2048.0, None, A.mult))
+        v("BA BB", "BC", 64, lambda: tt(D["BC"], D["BA"], D["BB"], A.add))
+        v("PI2", "BD", 64, lambda: ts(D["BD"], D["PI2"], 8.0, 8.0, A.is_ge, A.mult))
+        v("BC BD", "BE", 64, lambda: tt(D["BE"], D["BC"], D["BD"], A.add))
+        v("BW1 BE", "BW0", 64, lambda: ts(D["BW0"], D["BW1"], D["BE"], None, A.add))
+
+    def gather(out, base, off, r, tok):
+        for c in range(2048 // GC):
+            w = " ".join("%s.%d" % (tok, i) for i in range(c * GC // 512, (c + 1) * GC // 512))
+            s(r, w, GC * 1.5, lambda c=c: act(out[:, base + GC * c:base + GC * c + GC], X[:, 0:W].indirect(off[:, GC // 16 * c:GC // 16 * (c + 1)]), F.Copy))
+
+    def lanesum(wb, k, m, src, mov, start, stop, o=0):
+        return mm(wb[k][:, m:128:16], src[:, o + m:o + 2048:16], mov, start, stop)
+
+    def phase1(t, b):
+        x = str(b)
+        Vb, AD, wb, w_ = D["V" + x], D["AD" + x], WB[b], "W" + x
+        gather(Vb, 16, D["OFF" + x], "X OFF" + x, "V" + x)
+        for c in range(4):
+            j = 512 * c
+            i = lane()
+            p("V%s.%d %s IB NIB" % (x, c, "V%sz" % x if c == 0 else "V%s.%d" % (x, c - 1)), "L%d" % i, 1024,
+              lambda j=j, i=i: [mm(L[i][:], D["IB"], Vb[:, 16 + j:528 + j], True, False), mm(L[i][:], D["NIB"], Vb[:, 15 + j:527 + j], False, True)], ["L%d" % i])
+            s("L%d" % i, "AD%s.%d" % (x, c), 512, lambda j=j, i=i: act(AD[:, j:j + 512], L[i][:], F.Abs), ["L%d" % i])
+            i = lane()
+            p("AD%s.%d NB CL CR" % (x, c), "L%d" % i, 1024, lambda j=j, i=i: [mm(L[i][:], D["CL"], D["CR"], True, False), mm(L[i][:], D["NB"], AD[:, j:j + 512], False, True)], ["L%d" % i])
+            v("L%d V%s.%d" % (i, x, c), "Z%s.%d" % (x, c), 512, lambda j=j, i=i: sc(Z[:, 2048 * b + j:2048 * b + j + 512], L[i][:], Vb[:, 16 + j:528 + j], 0.0, A.min, A.max), ["L%d" % i])
+        p(" ".join("AD%s.%d" % (x, c) for c in range(4)) + " BIASC P4 B DEAD%s DE%sa" % (x, x), w_ + ".0", 1280,
+          lambda: [mm(wb[0], D["IB"], D["BIASC"], True, False), mm(wb[0], D["P4"], D["DEAD" + x], False, False)]
+          + [lanesum(wb, 0, m, AD, D["B"][:, 0:128:16], False, m == 15) for m in range(16)], [w_])
+        v(w_ + ".0", "S" + x, 128, lambda: ts(D["S" + x][:, :, 0:8], wb[0], 0.0, None, A.is_gt), [w_])
+        p("S%s S%s9 DEAD%s DE%sa IB NIB" % (x, x, x, x), w_ + ".1", 256, lambda: [mm(wb[1], D["IB"], D["S" + x][:, :, 1:9], True, False), mm(wb[1], D["NIB"], D["DEAD" + x], False, True)], [w_])
+
+    def runs(t, b):
+        x, y = str(b), "%d%d" % (t, b)
+        wb, w_, Sx = WB[b], "W" + x, D["S" + x][:, :, 0:8]
+        s("S%s K1" % x, "NS" + x, 128, lambda: act(D["NS" + x], Sx, F.Identity, bias=D["K1"], scale=-1.0))
+        s("S%s K2" % x, "SP" + x, 128, lambda: act(D["SP" + x], Sx, F.Identity, bias=D["K2"]))
+        v("NS%s SP%s" % (x, x), "C" + x, 64, lambda: sc(D["C" + x], D["NS" + x], D["SP" + x], 0.0, A.mult, A.add))
+        s("C%s CCT" % x, "CT" + x, 128, lambda: act(D["CT" + x], D["C" + x], F.Identity, bias=D["CCT"], scale=9776.0))
+        v(w_ + ".1 NK0", "CN" + x, 128, lambda: sc(D["CN" + x], D["NK0"], wb[1], 0.0, A.mult, A.add), [w_])
+        s("CN" + x, "MX" + y, 16, lambda: act(D["MX" + y], D["CN" + x][:, 7::8], F.Copy))
+        i = op("g", "MX" + y, "", 0.8, lambda: [send_counts(y)], sem="none")
+        op("r", "", "MR" + y, 0.0, None, sem="rm" + y, inc=len(count_engines(nxt, core)), after=[i], lat=3.0)
+
+    def upart(t, b):
+        x = str(b)
+        wb, w_ = WB[b], "W" + x
+        zs = " ".join("Z%s.%d" % (x, c) for c in range(4))
+        zo = 2048 * b
+        p(zs + " P4 C129 WM", w_ + ".2", 1200, lambda: [mm(wb[2], D["P4"], D["C129"], True, False)] + [lanesum(wb, 2, m, Z[:, zo:zo + 2048], D["WM"], False, m == 15) for m in range(16)], [w_])
+        p(zs + " P4 C128 WM", "UB%sa" % x, 1200, lambda: [mm(UB[b], D["P4"], D["C128"], True, False)] + [lanesum(UB, b, m, Z[:, zo:zo + 2048], D["WM"], False, False) for m in range(16)], ["UB"])
+        v(w_ + ".2", "KP" + x, 128, lambda: ts(D["KP" + x], wb[2], 1.0 / 4096, -0.5 + 1.0 / 8192, A.mult, A.add), [w_])
+        p("KP%s N4 UB%sa" % (x, x), "UB%s UB%sa" % (x, x), 128, lambda: [mm(UB[b], D["N4"], D["KP" + x], False, True)], ["UB"])
+        s("UB%s CSQ" % x, "SQ" + x, 128, lambda: act(UB[2 + b], UB[b], F.Square, bias=D["CSQ"]), ["UB"])
+
+    def hpart(t, b):
+        x = str(b)
+        v("SQ%s CT%s" % (x, x), "WI" + x, 128, lambda: tt(D["WI" + x], D["CT" + x], UB[2 + b], A.add), ["UB"])
+        v("WI" + x, "HI" + x, 128, lambda: ts(D["HI" + x], D["WI" + x], 5, 4095, A.arith_shift_right, A.bitwise_and))
+        v("HI" + x, "HF" + x, 128, lambda: copy(D["HF" + x], D["HI" + x]))
+        p("HF%s IDF" % x, "PTH", 512, lambda: [P.transpose(PT[:, 0:128], D["HF" + x], D["IDF"])], ["PT"])
+        v("PTH", "HOFF" + x, 128, lambda: copy(D["HOFF" + x], PT[:, 0:128]), ["PT"])
+
+    def first1(t, b):
+        x = str(b)
+        wb, w_, FS, M0 = WB[b], "W" + x, D["FS" + x], D["MO" + x][:, 0:128]
+        v("CN%s %s.1" % (x, w_), "CE" + x, 128, lambda: tt(D["CE" + x], D["CN" + x], wb[1], A.mult), [w_])
+        v("CE" + x, "MO%s.0" % x, 64, lambda: ts(M0, D["CE" + x], 1.0, None, A.is_equal))
+        v("MO%s.0 UB%s" % (x, x), "FS%sc" % x, 128, lambda: tt(FS[:, 128:256], M0, UB[b], A.mult), ["UB"])
+        p("HF%s IDF P16 P4 KA%s " % (x, x) + " ".join("KB.%d" % k for k in range(16)), w_ + ".2", 768,
+          lambda: [mm(wb[2], D["IDF"], D["HF" + x], True, False), mm(wb[2], D["P16"], D["KA" + x], False, False), mm(wb[2], D["P4"], D["KB"], False, True)], [w_])
+        v("MO%s.0 %s.2" % (x, w_), "FS%sa" % x, 128, lambda: tt(FS[:, 0:128], M0, wb[2], A.mult), [w_])
+        v("FR FS%sa FS%sc" % (x, x), "FO" + x, 256, lambda: sc(D["FO" + x], D["FR"], FS, 0.0, A.mult, A.add))
+        for q in range(4):
+            r = slice(32 * q, 32 * q + 32)
+            gg("FVM FO" + x, "FV%s%d" % (x, q), 0.24, lambda r=r, q=q: gcopy(D["FVM"][r, 4 * b + q::8], D["FO" + x][r, 7::8], 32))
+
+    def first2(t):
+        p(" ".join("FV%d%d" % (b, q) for b in (0, 1) for q in range(4)) + " ".join(" PR%d" % q for q in range(4)) + " P4 ONES", "PTL", 640,
+          lambda: [mm(PT[:, 256:288], D["FVM"][:, 0:128], D["PR32"], True, True), mm(PT[:, 288:320], D["P4"], D["ONES"][:, 0:32], True, False),
+                   mm(PT[:, 288:320], D["FVM"][:, 128:256], D["PR32"], False, True)], ["PT"])
+        LI, LQ = D["LI"], D["LQ"]
+        v("PTL", "LI", 64, lambda: copy(LI, PT[:, 256:320]), ["PT"])
+        v("LI", "L7", 64, lambda: ts(D["L7"], LI[:, 32:64], 4096 + 7, None, A.bitwise_and))
+        v("LI", "LQa", 64, lambda: ts(LQ[:, 0:32], LI[:, 0:32], 4095, None, A.bitwise_and))
+        v("LI", "LQb", 64, lambda: ts(LQ[:, 32:64], LI[:, 0:32], 12, None, A.arith_shift_right))
+        v("L7 BW0", "LQc", 64, lambda: tt(LQ[:, 64:96], D["L7"], D["BW0"], A.add))
+        v("LQa LQb LQc", "LOFF", 96, lambda: copy(D["LOFF"], LQ))
+
+    def update(t):
+        zs = " ".join("Z%d.%d" % (b, c) for b in (0, 1) for c in range(4))
+        s(zs + " LOFF KZ", "ZS", 512 * 1.5, lambda: act(D["ZS"], Z[:].indirect(D["LOFF"][:, 32:64]), F.Identity, bias=D["KZ"]))
+        v("X LOFF ZS", "ZX", 512 * 1.5, lambda: tt(D["ZX"], X[:, 0:W].indirect(D["LOFF"][:, 0:32]), D["ZS"], A.add))
+        v("ZX", "ZI", 256, lambda: ts(D["ZI"], D["ZX"], 0.5, -129.0, A.mult, A.add))
+        v("ZI LOFF", "X", 512 * 3.5, lambda: copy(X[:].indirect(D["LOFF"][:, 64:96]), D["ZI"]))
+
+    def phase2(t, b):
+        x = str(b)
+        XH, AE = D["XH" + x], D["AE" + x]
+        gather(XH, 0, D["HOFF" + x], "X HOFF" + x, "XH" + x)
+        for c in range(4):
+            j = 512 * c
+            i = lane()
+            p("XH%s.%d Z%s.%d IB NIB" % (x, c, x, c), "L%d" % i, 1024,
+              lambda j=j, i=i: [mm(L[i][:], D["NIB"], Z[:, 2048 * b + j:2048 * b + j + 512], True, False), mm(L[i][:], D["IB"], XH[:, j:j + 512], False, True)], ["L%d" % i])
+            s("L%d" % i, "AE%s.%d" % (x, c), 512, lambda j=j, i=i: act(AE[:, j:j + 512], L[i][:], F.Abs), ["L%d" % i])
+
+    def dpart(t, b):
+        x = str(b)
+        p(" ".join("AE%s.%d" % (x, c) for c in range(4)) + " B", "W%s.0" % x, 1024, lambda: [lanesum(WB[b], 0, m, D["AE" + x], D["B"][:, 0:128:16], True, True) for m in range(16)], ["W" + x])
+
+    def names1(t, b):
+        x, y = str(b), "%d%d" % (t, b)
+        wb, w_, MO, MV = WB[b], "W" + x, D["MO" + x], D["MV" + x]
+        v("S%s NM%s NM%sa" % (x, x, x), "SN" + x, 256, lambda: tt(D["SN" + x], D["S" + x][:, :, 0:8], D["NM" + x], A.mult))
+        v("NS%s SN%s" % (x, x), "AX" + x, 128, lambda: sc(D["AX" + x], D["NS" + x], D["SN" + x], 0.0, A.mult, A.add))
+        v("AX%s C%s" % (x, x), "T0" + x, 256, lambda: tt(D["T0" + x], D["C" + x], D["AX" + x], A.mult))
+        v("T0%s A4" % x, "TI" + x, 128, lambda: ts(D["TI" + x], D["T0" + x], D["A4"], 1024.0, A.add, A.mult))
+        v("TI" + x, "TJ" + x, 128, lambda: ts(D["TJ" + x], D["TI" + x], 4095 << 12, None, A.bitwise_and))
+        v("TJ" + x, "P1" + x, 128, lambda: ts(PV[:, 1 + b], D["TJ" + x], 1.0, None, A.add), ["PV"])
+        v("CE" + x, "CX" + x, 64, lambda: ts(D["CX" + x], D["CE" + x][:, :, 4:8], 4.5, None, A.max))
+        p("CX%s MR%s IB" % (x, y), w_ + ".3", 320, lambda: [mm(wb[3][:, 0:64], D["IB"], D["CX" + x], True, False)] + [mm(wb[3][:, k:64:4], D["IB"], D["MR" + y], False, k == 3) for k in range(4)], [w_])
+        for q in range(1, 4):
+            v("CE" + x, "MO%s.%d" % (x, q), 64, lambda q=q: ts(MO[:, 128 * q:128 * q + 128], D["CE" + x], q + 1.0, None, A.is_equal))
+        for q in range(4):
+            v(w_ + ".3", "MV%s.%d" % (x, q), 64, lambda q=q: ts(MV[:, 64 * q:64 * q + 64], wb[3][:, 0:64], q + 5.0, None, A.is_equal), [w_])
+
+    def names2(t, b):
+        x, y = str(b), "%d%d" % (t, b)
+        wb, w_, PRO, PRV = WB[b], "W" + x, D["PRO" + x], D["PRV" + x]
+        v(w_ + ".0 C" + x, "PV.0", 128, lambda: tt(PV[:, 0], D["C" + x], wb[0], A.mult), [w_, "PV"])
+        v("PV.0 HI" + x, "N2" + x, 128, lambda: tt(D["N2" + x], D["HI" + x], PV[:, 0], A.add), ["PV"])
+        v("N2" + x, "N3" + x, 128, lambda: ts(D["N3" + x], D["N2" + x], 4095, None, A.bitwise_and))
+        v("N3%s P1%s" % (x, x), "PV.3", 128, lambda: tt(PV[:, 3], D["N3" + x], PV[:, 1 + b], A.add), ["PV"])
+        for q in range(4):
+            v("MV%s.%d PV.3" % (x, q), "PRV%s.%d" % (x, q), 64, lambda q=q: tt(PRV[:, 64 * q:64 * q + 64], D["MV" + x][:, 64 * q:64 * q + 64], PV[:, 3, :, 4:8], A.mult), ["PV"])
+        v(" ".join("PRV%s.%d" % (x, q) for q in range(4)) + " CRV", "OSV" + x, 256, lambda: sc(D["OSV" + x], D["CRV"], PRV, 0.0, A.mult, A.add))
+        for q in range(4):
+            gg("OSV" + x, "SV%s.%d" % (y, q), 0.21, lambda q=q: gcopy(D["SV" + y][:, :, q], D["OSV" + x][:, 64 * q + 3:64 * q + 64:4], 16))
+        sv = " ".join("SV%s.%d" % (y, q) for q in range(4))
+        for k in (0, 2):
+            for q in (k, k + 1):
+                v("MO%s.%d PV.3" % (x, q), "PRO%s.%d" % (x, q), 128, lambda q=q: tt(PRO[:, 128 * q:128 * q + 128], D["MO" + x][:, 128 * q:128 * q + 128], PV[:, 3], A.mult), ["PV"])
+            r = slice(128 * k, 128 * k + 256)
+            v("PRO%s.%d PRO%s.%d CRO" % (x, k, x, k + 1), "OSO%s.%d" % (x, k), 256, lambda r=r: sc(D["OSO" + x][:, r], D["CRO"][:, r], PRO[:, r], 0.0, A.mult, A.add))
+            for q in (k, k + 1):
+                s("KM OSO%s.%d" % (x, k), "SO%s.%d" % (y, q), 64, lambda q=q: act(D["SO" + y][:, :, q], D["OSO" + x][:, 128 * q + 7:128 * q + 128:8], F.Identity, bias=D["KM"]))
+        so = " ".join("SO%s.%d" % (y, q) for q in range(4))
+        if t < NV - 1:
+            i = op("g", so + " " + sv, "", 0.8, lambda: [send_pairs(y)], sem="none")
+            op("r", "", "RO%s RV%s" % (y, y), 0.0, None, sem="rx" + y, inc=len(pair_engines(prv, core, 0)) + len(pair_engines(pr2, prv, 1)), after=[i], lat=3.5)
+        else:
+            i = op("g", sv, "", 0.8, lambda: [send_last(y)], sem="none")
+            op("r", "", "RV" + y, 0.0, None, sem="rx" + y, inc=len(count_engines(prv, core)), after=[i], lat=3.5)
+
+    def join(t, b):
+        x, y, last = str(b), "%d%d" % (t, b), t == NV - 1
+        J, NM, DE = D["J" + x], D["NM" + x], D["DEAD" + x]
+        own, ov = D[("SO" if last else "RO") + y], D["RV" + y]
+        rd = "RV%s " % y + (" ".join("SO%s.%d" % (y, q) for q in range(4)) if last else "RO" + y)
+        if last:
+            v(rd, "J" + x, 128, lambda: tt(J, own, ov, A.add))
+            jt = "J" + x
+        else:
+            v(rd, "J%sa" % x, 112, lambda: tt(J[:, 2:16, :], own[:, 0:14, :], ov[:, 0:14, :], A.add))
+            v(rd, "J%sb" % x, 64, lambda: tt(J[:, 0:2, :], own[:, 14:16, :], ov[:, 14:16, :], A.add))
+            jt = "J%sa J%sb" % (x, x)
+        jm, jn = J, jt
+        if last:
+            jm, jn = D["JM" + x], "JM" + x
+            v(jt, jn, 64, lambda: ts(jm, J, 0.0, None, A.max))
+        v(jn, "NM%sa" % x, 64, lambda: ts(NM[:, :, 0::2], jm, 12, None, A.arith_shift_right))
+        v(jn, "NM" + x, 64, lambda: ts(NM[:, :, 1::2], jm, 4095, None, A.bitwise_and))
+        v("NM%s NM%sa" % (x, x), "NF" + x, 128, lambda: copy(D["NF" + x], NM))
+        p("NF%s IDF" % x, "PTN", 512, lambda: [P.transpose(PT[:, 128:256], D["NF" + x], D["IDF"])], ["PT"])
+        if not last:
+            v("PTN", "OFF" + x, 128, lambda: copy(D["OFF" + x], PT[:, 128:256]), ["PT"])
+            v(jt, "DE%sa" % x, 64, lambda: ts(DE[:, :, 0::2], J, 0.0, None, A.is_lt))
+            v(jt, "DEAD" + x, 64, lambda: ts(DE[:, :, 1::2], J, 0.0, None, A.is_lt))
+        else:
+            s("PTN", "YL" + x, 128, lambda: act(D["YL" + x], PT[:, 128:256], F.Copy), ["PT"])
+            ld("y", "yl" + x, T.yl[:, 128 * b:128 * b + 128], D["YL" + x], "YL" + x, "yl" + x, 2.5)
+            v(jt, "NA" + x, 64, lambda: ts(D["NA" + x], J, 0.0, 2.0, A.is_ge, A.mult))
+            v("NA" + x, "NC" + x, 64, lambda: tt(D["NC" + x], D["NA" + x][:, :, 0:2], D["NA" + x][:, :, 2:4], A.add))
+            v("NC" + x, "NN" + x, 64, lambda: tt(D["NN" + x], D["NC" + x][:, :, 0], D["NC" + x][:, :, 1], A.add))
+            p("NN%s IDF" % x, "LN" + x, 1024, lambda: [P.transpose(L[0][0:8, 256 * b + w1:256 * b + 256:2], D["NN" + x][:, w1::2], D["IDF"]) for w1 in (0, 1)], ["L0"])
+
+    def total(t):
+        p("ONES MX%d0 MX%d1" % (t, t), "PTA", 128, lambda: [mm(PT[:, 288:304], D["ONES"], D["MX%d0" % t], True, False), mm(PT[:, 288:304], D["ONES"], D["MX%d1" % t], False, True)], ["PT"])
+        v("PTA", "AR", 64, lambda: V.tensor_reduce(D["AR"], PT[:, 288:304], AxisListType.X, A.add), ["PT"])
+        v("AR", "AI", 64, lambda: copy(D["AI"], D["AR"]))
+        v("AI", "AI2", 64, lambda: ts(D["AI2"], D["AI"], 255, None, A.bitwise_and))
+        v("AI2", "A4", 64, lambda: ts(D["A4"], D["AI2"], 4.0, None, A.mult))
+
+    def count_engines(a, c):
+        return topo.engines(a, c)[0:8]
+
+    def pair_engines(a, c, k):
+        e = topo.engines(a, c)
+        return (e[8:16], e[0:8])[k] if len(e) == 16 else (e[0:4], e[4:8])[k]
+
+    def mask(es):
+        return sum(1 << e for e in es)
+    lsum = [0]
+
+    def send_one(dst, out, in_, sem):
+        es = count_engines(core, dst)
+        rid, pid, _ = topo.addr(dst)
+        lsum[0] += len(es)
+        g.remote_dma(D[out], D[in_], T.sem[sem], T.sem.ls, pid, rid, mask(es))
+
+    def send_counts(y):
+        send_one(prv, "MR" + y, "MX" + y, "rm" + y)
+
+    def send_last(y):
+        send_one(nxt, "RV" + y, "SV" + y, "rx" + y)
+
+    def send_pairs(y):
+        tr = []
+        for k, dst, o, i in ((0, nxt, "RO", "SO"), (1, nx2, "RV", "SV")):
+            es = pair_engines(core, nxt, k)
+            lsum[0] += len(es)
+            rid, pid, _ = topo.addr(dst)
+            tr.append(RemoteDMATransfer(dst_ids=[DstId(rid=rid, pnc=pid)], dma_engine_mask=mask(es), remote_sem=T.sem["rx" + y], srcs=[D[i + y]], dsts=[D[o + y]]))
+        g.remote_dma_fused(tr, local_sem=T.sem.ls)
+
+    def part(key, fn, *a):
+        cur[0] = key + "".join(str(k) for k in a[1:])
+        fn(*a)
+        cur[0] = ""
+
+    for t in range(NV):
+        for b in (0, 1):
+            part("phase1", phase1, t, b)
+            part("runs", runs, t, b)
+            part("upart", upart, t, b)
+            part("hpart", hpart, t, b)
+        if t == 0:
+            late_constants()
+        for b in (0, 1):
+            part("phase2", phase2, t, b)
+            part("first1", first1, t, b)
+            part("names1", names1, t, b)
+        part("first2", first2, t)
+        part("update", update, t)
+        if t == NV - 1:
+            ld("y", "yx", T.yx[:], X[:, 0:W], "X", "yx", 7.0)
+        for b in (0, 1):
+            part("dpart", dpart, t, b)
+            part("names2", names2, t, b)
+        if t < NV - 1:
+            total(t)
+        for b in (0, 1):
+            part("join", join, t, b)
+    v("LN0 LN1", "YN", 512, lambda: copy(D["YN"], L[0][0:8, :]), ["L0"])
+    ld("y", "yn", T.yn[:], D["YN"], "YN", "yn", 2.5)
+    emit(g, T, ops)
+    g.wait_ge(T.sem.ls, lsum[0])
+
+
+BOOST = {"phase11v": 70, "names20v": -7, "phase20p": -92, "first2p": 30, "phase10p": 13, "upart0p": 60, "updates": 27, "names11v": -8, "runs1s": 38}
+
+
+def emit(g, T, ops):
+    deps = links(ops)
+    issue(g, T, ops, deps, arrange(ops, deps, BOOST, HOP)[0])
+
+
+def links(ops):
+    N = len(ops)
+    lastw, readers, banks = {}, {}, {}
+    deps = [dict() for _ in range(N)]
+
+    def add(i, j, hard):
+        if j != i:
+            deps[i][j] = deps[i].get(j, False) or hard
+    for i, o in enumerate(ops):
+        for k in o["r"]:
+            if k in lastw:
+                add(i, lastw[k], True)
+            readers.setdefault(k, []).append(i)
+        for k in o["w"]:
+            if k in lastw:
+                add(i, lastw[k], True)
+            for j in readers.get(k, []):
+                add(i, j, True)
+            lastw[k] = i
+            readers[k] = []
+        for k in o["b"]:
+            for j in banks.get(k, []):
+                add(i, j, ops[j]["q"] != o["q"])
+            banks.setdefault(k, []).append(i)
+        for j in o["after"]:
+            add(i, j, False)
+    return deps
+
+
+def arrange(ops, deps, boost, hop):
+    N = len(ops)
+    succ = [[] for _ in range(N)]
+    for i in range(N):
+        for j in deps[i]:
+            succ[j].append(i)
+    prio = [0.0] * N
+    for i in range(N - 1, -1, -1):
+        o = ops[i]
+        prio[i] = o["cost"] + o["lat"] + max([prio[j] + hop for j in succ[i]] or [0.0])
+    prio = [prio[i] + boost.get(ops[i]["k"], 0.0) for i in range(N)]
+    left = [len(deps[i]) for i in range(N)]
+    ready = [0.0] * N
+    free, cand, order = {}, {}, []
+    for i in range(N):
+        if left[i] == 0:
+            cand.setdefault(ops[i]["q"], []).append(i)
+    while len(order) < N:
+        best = None
+        for q in sorted(cand):
+            if cand[q]:
+                st = max(free.get(q, 0.0), min(ready[i] for i in cand[q]))
+                if best is None or st < best[0]:
+                    best = (st, q)
+        st, q = best
+        i = max((i for i in cand[q] if ready[i] <= st + 1e-9), key=lambda i: (prio[i], -i))
+        cand[q].remove(i)
+        order.append(i)
+        end = st + ops[i]["cost"]
+        if q != "r":
+            free[q] = end
+        end += ops[i]["lat"]
+        for j in succ[i]:
+            ready[j] = max(ready[j], end + (hop if deps[j][i] and q != "r" else 0.0))
+            left[j] -= 1
+            if left[j] == 0:
+                cand.setdefault(ops[j]["q"], []).append(j)
+    return order, max(free.values())
+
+
+def issue(g, T, ops, deps, order):
+    queues = {"v": g.vector, "s": g.scalar, "d": g.scalar, "p": g.tensor, "g": g, "y": g.sync}
+    sems = {"v": "qv", "s": "qs", "p": "qp", "g": "qg"}
+    level, done, seen = {}, {}, {}
+    for i in order:
+        o = ops[i]
+        q = o["q"]
+        if q == "r":
+            level[o["sem"]] = level.get(o["sem"], 0) + o["inc"]
+            done[i] = (o["sem"], level[o["sem"]])
+            continue
+        qk = "s" if q == "d" else q
+        need = {}
+        for j, hard in deps[i].items():
+            if hard and done[j] is not None:
+                sm, c = done[j]
+                need[sm] = max(need.get(sm, 0), c)
+        for sm in sorted(need):
+            if seen.get((qk, sm), 0) < need[sm]:
+                seen[(qk, sm)] = need[sm]
+                queues[q].wait_ge(T.sem[sm], need[sm])
+        res = o["fn"]()
+        if o["sem"] == "none":
+            done[i] = None
+            continue
+        sm, inc = (o["sem"], o["inc"]) if o["sem"] else (sems[q], 1)
+        for r in res:
+            r.then_inc(T.sem[sm], inc)
+            level[sm] = level.get(sm, 0) + inc
+        done[i] = (sm, level[sm])
+    for sm in sorted(level):
+        if seen.get(("g", sm), 0) < level[sm]:
+            g.wait_ge(T.sem[sm], level[sm])

@@ -2,7 +2,8 @@ from concourse.bass import DstId, RemoteDMATransfer
 from concourse.mybir import dt, AluOpType, AxisListType, ActivationFunctionType
 
 NV, W = 3, 4096
-GC = 1024
+CALLS1 = [[("s", 0, 1), ("v", 1, 2), ("s", 2, 3), ("v", 3, 4)], [("s", 0, 2), ("s", 2, 4)]]
+CALLS2 = [[("s", 0, 2), ("s", 2, 4)], [("s", 0, 2), ("s", 2, 4)]]
 BFT, F32, I32, U16 = "bfloat16", "float32", "int32", "uint16"
 SCRATCH = {}
 VIEWS = {}
@@ -181,10 +182,14 @@ def rank_program(g, core, T, topo):
         v("BC BD", "BE", 64, lambda: tt(D["BE"], D["BC"], D["BD"], A.add))
         v("BW1 BE", "BW0", 64, lambda: ts(D["BW0"], D["BW1"], D["BE"], None, A.add))
 
-    def gather(out, base, off, r, tok):
-        for c in range(2048 // GC):
-            w = " ".join("%s.%d" % (tok, i) for i in range(c * GC // 512, (c + 1) * GC // 512))
-            s(r, w, GC * 1.5, lambda c=c: act(out[:, base + GC * c:base + GC * c + GC], X[:, 0:W].indirect(off[:, GC // 16 * c:GC // 16 * (c + 1)]), F.Copy))
+    def gather(out, base, off, r, tok, calls):
+        for q, a, e in calls:
+            w = " ".join("%s.%d" % (tok, i) for i in range(a, e))
+            o, x = out[:, base + 512 * a:base + 512 * e], off[:, 32 * a:32 * e]
+            if q == "s":
+                s(r, w, (e - a) * 512 * 1.5, lambda o=o, x=x: act(o, X[:, 0:W].indirect(x), F.Copy))
+            else:
+                v(r, w, (e - a) * 512 * 1.5, lambda o=o, x=x: copy(o, X[:, 0:W].indirect(x)))
 
     def lanesum(wb, k, m, src, mov, start, stop, o=0):
         return mm(wb[k][:, m:128:16], src[:, o + m:o + 2048:16], mov, start, stop)
@@ -192,7 +197,7 @@ def rank_program(g, core, T, topo):
     def phase1(t, b):
         x = str(b)
         Vb, AD, wb, w_ = D["V" + x], D["AD" + x], WB[b], "W" + x
-        gather(Vb, 16, D["OFF" + x], "X OFF" + x, "V" + x)
+        gather(Vb, 16, D["OFF" + x], "X OFF" + x, "V" + x, CALLS1[b])
         for c in range(4):
             j = 512 * c
             i = lane()
@@ -200,11 +205,12 @@ def rank_program(g, core, T, topo):
               lambda j=j, i=i: [mm(L[i][:], D["IB"], Vb[:, 16 + j:528 + j], True, False), mm(L[i][:], D["NIB"], Vb[:, 15 + j:527 + j], False, True)], ["L%d" % i])
             s("L%d" % i, "AD%s.%d" % (x, c), 512, lambda j=j, i=i: act(AD[:, j:j + 512], L[i][:], F.Abs), ["L%d" % i])
             i = lane()
-            p("AD%s.%d NB CL CR" % (x, c), "L%d" % i, 1024, lambda j=j, i=i: [mm(L[i][:], D["CL"], D["CR"], True, False), mm(L[i][:], D["NB"], AD[:, j:j + 512], False, True)], ["L%d" % i])
+            p("CL CR", "L%d" % i, 512, lambda i=i: [mm(L[i][:], D["CL"], D["CR"], True, False)], ["L%d" % i])
+            p("AD%s.%d NB" % (x, c), "L%d" % i, 512, lambda j=j, i=i: [mm(L[i][:], D["NB"], AD[:, j:j + 512], False, True)], ["L%d" % i])
             v("L%d V%s.%d" % (i, x, c), "Z%s.%d" % (x, c), 512, lambda j=j, i=i: sc(Z[:, 2048 * b + j:2048 * b + j + 512], L[i][:], Vb[:, 16 + j:528 + j], 0.0, A.min, A.max), ["L%d" % i])
-        p(" ".join("AD%s.%d" % (x, c) for c in range(4)) + " BIASC P4 B DEAD%s DE%sa" % (x, x), w_ + ".0", 1280,
-          lambda: [mm(wb[0], D["IB"], D["BIASC"], True, False), mm(wb[0], D["P4"], D["DEAD" + x], False, False)]
-          + [lanesum(wb, 0, m, AD, D["B"][:, 0:128:16], False, m == 15) for m in range(16)], [w_])
+        p("IB BIASC P4 DEAD%s DE%sa" % (x, x), w_ + ".0", 256, lambda: [mm(wb[0], D["IB"], D["BIASC"], True, False), mm(wb[0], D["P4"], D["DEAD" + x], False, False)], [w_])
+        p(" ".join("AD%s.%d" % (x, c) for c in range(4)) + " B", w_ + ".0", 1024,
+          lambda: [lanesum(wb, 0, m, AD, D["B"][:, 0:128:16], False, m == 15) for m in range(16)], [w_])
         v(w_ + ".0", "S" + x, 128, lambda: ts(D["S" + x][:, :, 0:8], wb[0], 0.0, None, A.is_gt), [w_])
         p("S%s S%s9 DEAD%s DE%sa IB NIB" % (x, x, x, x), w_ + ".1", 256, lambda: [mm(wb[1], D["IB"], D["S" + x][:, :, 1:9], True, False), mm(wb[1], D["NIB"], D["DEAD" + x], False, True)], [w_])
 
@@ -275,12 +281,12 @@ def rank_program(g, core, T, topo):
     def phase2(t, b):
         x = str(b)
         XH, AE = D["XH" + x], D["AE" + x]
-        gather(XH, 0, D["HOFF" + x], "X HOFF" + x, "XH" + x)
+        gather(XH, 0, D["HOFF" + x], "X HOFF" + x, "XH" + x, CALLS2[b])
         for c in range(4):
             j = 512 * c
             i = lane()
-            p("XH%s.%d Z%s.%d IB NIB" % (x, c, x, c), "L%d" % i, 1024,
-              lambda j=j, i=i: [mm(L[i][:], D["NIB"], Z[:, 2048 * b + j:2048 * b + j + 512], True, False), mm(L[i][:], D["IB"], XH[:, j:j + 512], False, True)], ["L%d" % i])
+            p("Z%s.%d NIB" % (x, c), "L%d" % i, 512, lambda j=j, i=i: [mm(L[i][:], D["NIB"], Z[:, 2048 * b + j:2048 * b + j + 512], True, False)], ["L%d" % i])
+            p("XH%s.%d IB" % (x, c), "L%d" % i, 512, lambda j=j, i=i: [mm(L[i][:], D["IB"], XH[:, j:j + 512], False, True)], ["L%d" % i])
             s("L%d" % i, "AE%s.%d" % (x, c), 512, lambda j=j, i=i: act(AE[:, j:j + 512], L[i][:], F.Abs), ["L%d" % i])
 
     def dpart(t, b):
@@ -314,6 +320,9 @@ def rank_program(g, core, T, topo):
             v("MV%s.%d PV.3" % (x, q), "PRV%s.%d" % (x, q), 64, lambda q=q: tt(PRV[:, 64 * q:64 * q + 64], D["MV" + x][:, 64 * q:64 * q + 64], PV[:, 3, :, 4:8], A.mult), ["PV"])
         v(" ".join("PRV%s.%d" % (x, q) for q in range(4)) + " CRV", "OSV" + x, 256, lambda: sc(D["OSV" + x], D["CRV"], PRV, 0.0, A.mult, A.add))
         for q in range(4):
+            if b:
+                s("OSV" + x, "SV%s.%d" % (y, q), 64, lambda q=q: act(D["SV" + y][:, :, q], D["OSV" + x][:, 64 * q + 3:64 * q + 64:4], F.Copy))
+                continue
             gg("OSV" + x, "SV%s.%d" % (y, q), 0.21, lambda q=q: gcopy(D["SV" + y][:, :, q], D["OSV" + x][:, 64 * q + 3:64 * q + 64:4], 16))
         sv = " ".join("SV%s.%d" % (y, q) for q in range(4))
         for k in (0, 2):
@@ -436,7 +445,8 @@ def rank_program(g, core, T, topo):
     g.wait_ge(T.sem.ls, lsum[0])
 
 
-BOOST = {"phase11v": 70, "names20v": -7, "phase20p": -92, "first2p": 30, "phase10p": 13, "upart0p": 60, "updates": 27, "names11v": -8, "runs1s": 38}
+BOOST = {"runs1s": 258, "first2v": 246, "phase21p": -108, "names11v": -14, "phase10v": 32, "phase21s": -140, "upart1s": 138, "first11v": -82,
+         "first10v": -16, "runs0s": 196, "phase20p": -122, "first10p": -102, "phase11p": -84}
 
 
 def emit(g, T, ops):
@@ -459,7 +469,7 @@ def links(ops):
             readers.setdefault(k, []).append(i)
         for k in o["w"]:
             if k in lastw:
-                add(i, lastw[k], True)
+                add(i, lastw[k], not (o["q"] == "p" and ops[lastw[k]]["q"] == "p"))
             for j in readers.get(k, []):
                 add(i, j, True)
             lastw[k] = i

from concourse.bass import DstId, RemoteDMATransfer
from concourse.mybir import dt, AluOpType, AxisListType, ActivationFunctionType

NV, W = 3, 4096
CALLS1 = [[("s", 0, 1), ("v", 1, 2), ("s", 2, 3), ("v", 3, 4)], [("s", 0, 2), ("s", 2, 4)]]
CALLS2 = [[("s", 0, 2), ("s", 2, 4)], [("s", 0, 2), ("s", 2, 4)]]
BFT, F32, I32, U16 = "bfloat16", "float32", "int32", "uint16"
SCRATCH = {}
VIEWS = {}


def _sb(name, shape, ty):
    buf = "b_" + "_".join(str(n) for n in shape) + "_" + ty
    k = SCRATCH[buf][1][1] if buf in SCRATCH else 0
    SCRATCH[buf] = ("sbuf", [shape[0], k + 1] + shape[1:], ty)
    VIEWS[name] = (buf, k)


SCRATCH["X"] = ("sbuf", [128, 8192], BFT)
SCRATCH["Z"] = ("sbuf", [128, 4096], BFT)
for _n in ("L0", "L1", "L2", "PT", "W0", "W1", "UB"):
    SCRATCH[_n] = ("psum", [128, 512], F32)
SCRATCH["PV"] = ("psum", [128, 4, 16, 8], F32)
for _n, _s, _t in (
        ("ONES", [128, 128], BFT), ("B1", [128, 128], BFT), ("B", [128, 128], BFT), ("IB", [128, 128], BFT), ("NIB", [128, 128], BFT),
        ("NB", [128, 128], BFT), ("N4", [128, 128], BFT), ("P4", [128, 128], BFT), ("P16", [128, 128], BFT), ("CL", [128, 128], BFT),
        ("CR", [128, 512], BFT), ("IDF", [128, 128], F32), ("PR32", [128, 32], F32), ("E81", [8, 128], BFT), ("E8", [8, 128], BFT),
        ("BIASC", [128, 16, 8], BFT), ("WM", [128, 8], BFT), ("KA0", [128, 16, 8], BFT), ("KA1", [128, 16, 8], BFT), ("KB", [128, 16, 8], BFT),
        ("NK0", [128, 128], BFT), ("C129", [128, 16, 8], BFT), ("C128", [128, 16, 8], BFT),
        ("FR", [128, 256], F32), ("CRO", [128, 512], F32), ("CRV", [128, 256], F32), ("THB", [8, 1], BFT), ("THF", [8, 1], F32), ("DT", [8, 8], BFT),
        ("PID", [128, 1], I32), ("PI2", [128, 1], I32), ("WT", [128, 4], I32), ("AI", [128, 1], I32), ("AI2", [128, 1], I32), ("BX", [128, 1], I32), ("BY", [128, 1], I32),
        ("NZ", [128, 1], F32), ("COEF", [128, 1], F32), ("WCOL", [128, 1], F32), ("AR", [128, 1], F32), ("A4", [128, 1], F32), ("CSQ", [128, 1], F32), ("CCT", [128, 1], F32),
        ("K1", [128, 1], F32), ("K2", [128, 1], F32), ("KM", [128, 1], F32), ("KZ", [128, 1], F32), ("PF0", [128, 1], F32), ("PF1", [128, 1], F32), ("BA", [128, 1], F32), ("BB", [128, 1], F32), ("BC", [128, 1], F32),
        ("BD", [128, 1], F32), ("BE", [128, 1], F32), ("TH", [8, 1], I32), ("WN", [8, 512], I32), ("WNF", [8, 512], F32), ("WL", [128, 256], I32),
        ("BW1", [128, 32], I32), ("BW0", [128, 32], I32), ("L7", [128, 32], I32), ("FVM", [128, 256], F32), ("LI", [128, 64], I32), ("LQ", [128, 96], I32),
        ("LOFF", [128, 96], U16), ("ZS", [128, 512], F32), ("ZX", [128, 512], BFT), ("ZI", [128, 512], BFT), ("YN", [8, 512], F32)):
    _sb(_n, _s, _t)
for _b in "01":
    for _n, _s, _t in (
            ("V", [128, 2064], BFT), ("AD", [128, 2048], BFT), ("XH", [128, 2048], BFT), ("AE", [128, 2048], BFT),
            ("OFF", [128, 128], U16), ("HOFF", [128, 128], U16), ("DEAD", [128, 16, 8], BFT), ("NM", [128, 16, 8], I32), ("NF", [128, 128], F32),
            ("S", [128, 16, 9], BFT), ("NS", [128, 128], BFT), ("SP", [128, 128], BFT), ("C", [128, 128], BFT), ("CN", [128, 128], BFT), ("CE", [128, 16, 8], BFT),
            ("CX", [128, 16, 4], BFT), ("SN", [128, 128], F32), ("AX", [128, 128], F32), ("T0", [128, 16, 8], F32), ("TI", [128, 16, 8], I32), ("TJ", [128, 16, 8], I32),
            ("KP", [128, 16, 8], BFT), ("CT", [128, 16, 8], F32), ("WI", [128, 16, 8], I32), ("HI", [128, 16, 8], I32), ("HF", [128, 128], F32),
            ("FS", [128, 256], F32), ("FO", [128, 256], F32),
            ("MO", [128, 512], BFT), ("MV", [128, 256], BFT), ("N2", [128, 16, 8], I32), ("N3", [128, 16, 8], I32),
            ("PRO", [128, 512], F32), ("PRV", [128, 256], F32), ("OSO", [128, 512], F32), ("OSV", [128, 256], F32),
            ("J", [128, 16, 4], I32), ("JM", [128, 16, 4], I32), ("YL", [128, 128], F32), ("NA", [128, 16, 4], F32), ("NC", [128, 16, 2], F32), ("NN", [128, 16], F32)):
        _sb(_n + _b, _s, _t)
    for _i in range(NV):
        for _n in ("SO", "SV", "RO", "RV"):
            _sb("%s%d%s" % (_n, _i, _b), [128, 16, 4], F32)
        for _n in ("MX", "MR"):
            _sb("%s%d%s" % (_n, _i, _b), [128, 16], BFT)

DMAS = ["xv", "wl", "wn", "wt", "th", "yx", "yl0", "yl1", "yn"]
SEMAPHORES = ["qv", "qs", "qp", "qg", "ls"] + ["d_" + n for n in DMAS] + ["r%s%d%d" % (k, t, b) for k in "xm" for t in range(NV) for b in (0, 1)]
CY = 0.00104
PC = 0.00052
HOP = 0.08


def rank_program(g, core, T, topo):
    rank = T.rank_of(core)
    if rank is None:
        return
    n = len(T.cores)
    nxt, nx2, prv, pr2 = [T.cores[(rank + k) % n] for k in (1, 2, -1, -2)]
    A, F = AluOpType, ActivationFunctionType
    V, S, P = g.vector, g.scalar, g.tensor
    D = {k: T[b][:, i] for k, (b, i) in VIEWS.items()}
    X, Z, PT, PV, L = T.X, T.Z, T.PT, T.PV, [T.L0, T.L1, T.L2]
    tiles = [slice(128 * k, 128 * k + 128) for k in range(4)]
    UB, WB = [T.UB[:, k] for k in tiles], [[w[:, k] for k in tiles] for w in (T.W0, T.W1)]
    tt, mm, sc, act, mset, copy = V.tensor_tensor, P.matmul, V.tensor_tensor_scan, S.activation, V.memset, V.tensor_copy
    ops, cur = [], [""]

    def op(q, r, w, cost, fn, b=(), sem=None, inc=0, after=(), lat=0.0):
        ops.append({"k": cur[0] + q if cur[0] else "", "q": q, "r": r.split(), "w": w.split(), "cost": cost, "fn": fn, "b": list(b), "sem": sem, "inc": inc, "after": list(after), "lat": lat})
        return len(ops) - 1

    def v(r, w, cyc, fn, b=()):
        return op("v", r, w, 0.03 + CY * max(cyc, 64), lambda: [fn()], b)

    def s(r, w, cyc, fn, b=()):
        return op("s", r, w, 0.03 + CY * max(cyc, 64), lambda: [fn()], b)

    def p(r, w, cyc, fn, b):
        return op("p", r, w, PC * cyc, fn, b)

    def gg(r, w, cost, fn):
        return op("g", r, w, cost, lambda: [fn()])

    def ld(q, name, out, in_, r, w, cost):
        return op(q, r, w, 0.06, lambda: [(g.sync if q == "y" else S).dma_start(out, in_)], sem="d_" + name, inc=16, lat=cost)

    def ts(out, in0, s1, s2, o0, o1=None):
        if o1 is None:
            return V.tensor_scalar(out, in0, s1, None, o0)
        return V.tensor_scalar(out, in0, s1, s2, o0, o1)

    def gcopy(out, in_, n):
        return g.affine_select(out, in_, [[0, n]], A.is_equal, 0.0, 0, 0)

    nl = [0]

    def lane():
        nl[0] += 1
        return (nl[0] - 1) % len(L)

    ld("y", "wl", D["WL"], T.wl[:], "", "WL", 2.0)
    ld("y", "xv", X[:, 0:W], T.xv[:], "", "X", 7.0)
    ld("d", "th", D["TH"], T.th[:], "", "TH", 2.0)
    ld("d", "wt", D["WT"][:, 0:1], T.wt[:], "", "WT", 2.0)
    ld("d", "wn", D["WN"], T.wn[:], "", "WN", 2.0)
    v("", "ONES", 64, lambda: mset(D["ONES"], 1.0))
    gg("ONES", "B1", 0.5, lambda: g.affine_select(D["B1"], D["ONES"], [[-16, 8], [0, 16]], A.is_ge, 0.0, 0, 1))
    gg("B1", "B", 0.5, lambda: g.affine_select(D["B"], D["B1"], [[16, 8], [0, 16]], A.is_ge, 0.0, 15, -1))
    gg("ONES", "IB", 0.5, lambda: g.affine_select(D["IB"], D["ONES"], [[-1, 128]], A.is_equal, 0.0, 0, 1))
    gg("ONES", "E81", 0.5, lambda: g.affine_select(D["E81"], T.b_128_128_bfloat16[0:8, VIEWS["ONES"][1]], [[1, 128]], A.is_ge, 0.0, 0, -16))
    gg("E81", "E8", 0.5, lambda: g.affine_select(D["E8"], D["E81"], [[-1, 128]], A.is_ge, 0.0, 15, 16))
    gg("", "PID", 0.2, lambda: g.iota(D["PID"], [[0, 1]], 0, 1))
    gg("", "BW1", 0.3, lambda: g.iota(D["BW1"], [[16, 32]], 0, 0))
    for b in (0, 1):
        v("WL", "OFF%d" % b, 128, lambda b=b: copy(D["OFF%d" % b], D["WL"][:, 128 * b:128 * b + 128]))
        v("", "V%dz" % b, 64, lambda b=b: mset(D["V%d" % b][:, 0:16], 0.0))
        v("", "S%d9" % b, 64, lambda b=b: mset(D["S%d" % b][:, :, 8], 1.0))
    v("IB", "IDF", 128, lambda: copy(D["IDF"], D["IB"]))
    for k, src, c in (("NIB", "IB", -1.0), ("NB", "B", -16.0), ("N4", "IB", -4096.0), ("P4", "IB", 4096.0), ("P16", "IB", 65536.0)):
        v(src, k, 64, lambda k=k, src=src, c=c: ts(D[k], D[src], c, None, A.mult))
    v("", "CRa", 256, lambda: mset(D["CR"], 1.0))
    v("CRa", "CR", 64, lambda: mset(D["CR"][:, 0:512:8], -64.0))
    v("TH", "THB", 64, lambda: copy(D["THB"], D["TH"]))
    v("TH", "THF", 64, lambda: copy(D["THF"], D["TH"]))
    v("PID", "PI2", 64, lambda: ts(D["PI2"], D["PID"], 15, None, A.bitwise_and))
    v("PI2", "NZ", 64, lambda: ts(D["NZ"], D["PI2"], 0.0, None, A.is_gt))
    p("E8 THB", "PTth", 64, lambda: [mm(PT[:, 304:305], D["E8"], D["THB"], True, True)], ["PT"])
    v("PTth NZ", "COEF", 64, lambda: tt(D["COEF"], PT[:, 304:305], D["NZ"], A.add), ["PT"])
    v("B COEF", "CL", 64, lambda: ts(D["CL"], D["B"], D["COEF"], None, A.mult))
    v("THF IB", "DT", 64, lambda: ts(D["DT"], D["IB"][0:8, 0:8], D["THF"], None, A.mult))
    p("ONES DT", "W0.0", 1024, lambda: [mm(WB[0][0][:, m:128:16], D["ONES"][0:8, :], D["DT"], True, True) for m in range(16)], ["W0"])
    v("W0.0", "BIa", 128, lambda: ts(D["BIASC"], WB[0][0], -1.0, None, A.mult), ["W0"])
    v("BIa", "BIASC", 64, lambda: mset(D["BIASC"][:, :, 0], 8192.0))
    v("WT", "WCOL", 64, lambda: copy(D["WCOL"], D["WT"][:, 0:1]))
    v("B WCOL", "WM", 64, lambda: ts(D["WM"], D["B"][:, 0:128:16], D["WCOL"], None, A.mult))
    for k, c in (("C129", 129.0), ("C128", 128.0), ("A4", 0.0), ("CSQ", 4096.0 + 592.0), ("CCT", -360240.0), ("K1", 1.0), ("K2", 2.0), ("KM", -1.0), ("KZ", 257.5)):
        v("", k, 64, lambda k=k, c=c: mset(D[k], c))
    v("", "NKa", 64, lambda: mset(D["NK0"], 1.0))
    v("NKa", "NK0", 64, lambda: mset(D["NK0"][:, 0::8], 0.0))
    v("WN", "WNF", 512, lambda: copy(D["WNF"], D["WN"]))
    for b in (0, 1):
        p("WNF IDF", "PTn%d" % b, 512, lambda b=b: [P.transpose(PT[:, 320 + 16 * b + w1:336 + 16 * b:2], D["WNF"][:, 256 * b + w1:256 * b + 256:2], D["IDF"][0:8, 0:8]) for w1 in (0, 1)], ["PT"])
        for k in range(8):
            v("PTn%d" % b + (" " + " ".join("DE%d%d" % (b, i) for i in range(7)) if k == 7 else ""), "DEAD%d" % b if k == 7 else "DE%d%d" % (b, k), 64,
              lambda b=b, k=k: ts(D["DEAD%d" % b][:, :, k], PT[:, 320 + 16 * b:336 + 16 * b], float(k), None, A.is_le), ["PT"])
        v("WL", "NF%d" % b, 128, lambda b=b: copy(D["NF%d" % b], D["WL"][:, 128 * b:128 * b + 128]))
        p("NF%d IDF" % b, "PTN", 512, lambda b=b: [P.transpose(PT[:, 128:256], D["NF%d" % b], D["IDF"])], ["PT"])
        v("PTN", "NM%d" % b, 128, lambda b=b: copy(D["NM%d" % b], PT[:, 128:256]), ["PT"])

    def late_constants():
        v("", "FRa", 256, lambda: mset(D["FR"], 1.0))
        v("FRa", "FR", 64, lambda: mset(D["FR"][:, 0::8], 0.0))
        v("", "CROa", 512, lambda: mset(D["CRO"], 1.0))
        v("CROa", "CRO", 64, lambda: mset(D["CRO"][:, 0::8], 0.0))
        v("", "CRVa", 256, lambda: mset(D["CRV"], 1.0))
        v("CRVa", "CRV", 64, lambda: mset(D["CRV"][:, 0::4], 0.0))
        v("", "FVM", 256, lambda: mset(D["FVM"], 0.0))
        v("PID", "PF0", 64, lambda: copy(D["PF0"], D["PID"]))
        v("PF0", "PF1", 64, lambda: ts(D["PF1"], D["PF0"], 128.0, None, A.add))
        for b in (0, 1):
            v("PF%d C129" % b, "KA%d" % b, 64, lambda b=b: ts(D["KA%d" % b], D["C129"], 0.0, D["PF%d" % b], A.mult, A.add))
        for k in range(16):
            v("", "KB.%d" % k, 64, lambda k=k: mset(D["KB"][:, k // 8::2, k % 8], float(k)))
        for q in range(4):
            v("IDF", "PR%d" % q, 64, lambda q=q: copy(D["PR32"][32 * q:32 * q + 32, :], D["IDF"][32 * q:32 * q + 32, 32 * q:32 * q + 32]))
        v("PI2", "BX", 64, lambda: ts(D["BX"], D["PI2"], 3, None, A.bitwise_and))
        v("PI2", "BY", 64, lambda: ts(D["BY"], D["PI2"], 2, 1, A.arith_shift_right, A.bitwise_and))
        v("BX", "BA", 64, lambda: ts(D["BA"], D["BX"], 512.0, None, A.mult))
        v("BY", "BB", 64, lambda: ts(D["BB"], D["BY"], 2048.0, None, A.mult))
        v("BA BB", "BC", 64, lambda: tt(D["BC"], D["BA"], D["BB"], A.add))
        v("PI2", "BD", 64, lambda: ts(D["BD"], D["PI2"], 8.0, 8.0, A.is_ge, A.mult))
        v("BC BD", "BE", 64, lambda: tt(D["BE"], D["BC"], D["BD"], A.add))
        v("BW1 BE", "BW0", 64, lambda: ts(D["BW0"], D["BW1"], D["BE"], None, A.add))

    def gather(out, base, off, r, tok, calls):
        for q, a, e in calls:
            w = " ".join("%s.%d" % (tok, i) for i in range(a, e))
            o, x = out[:, base + 512 * a:base + 512 * e], off[:, 32 * a:32 * e]
            if q == "s":
                s(r, w, (e - a) * 512 * 1.5, lambda o=o, x=x: act(o, X[:, 0:W].indirect(x), F.Copy))
            else:
                v(r, w, (e - a) * 512 * 1.5, lambda o=o, x=x: copy(o, X[:, 0:W].indirect(x)))

    def lanesum(wb, k, m, src, mov, start, stop, o=0):
        return mm(wb[k][:, m:128:16], src[:, o + m:o + 2048:16], mov, start, stop)

    def phase1(t, b):
        x = str(b)
        Vb, AD, wb, w_ = D["V" + x], D["AD" + x], WB[b], "W" + x
        gather(Vb, 16, D["OFF" + x], "X OFF" + x, "V" + x, CALLS1[b])
        for c in range(4):
            j = 512 * c
            i = lane()
            p("V%s.%d %s IB NIB" % (x, c, "V%sz" % x if c == 0 else "V%s.%d" % (x, c - 1)), "L%d" % i, 1024,
              lambda j=j, i=i: [mm(L[i][:], D["IB"], Vb[:, 16 + j:528 + j], True, False), mm(L[i][:], D["NIB"], Vb[:, 15 + j:527 + j], False, True)], ["L%d" % i])
            s("L%d" % i, "AD%s.%d" % (x, c), 512, lambda j=j, i=i: act(AD[:, j:j + 512], L[i][:], F.Abs), ["L%d" % i])
            i = lane()
            p("CL CR", "L%d" % i, 512, lambda i=i: [mm(L[i][:], D["CL"], D["CR"], True, False)], ["L%d" % i])
            p("AD%s.%d NB" % (x, c), "L%d" % i, 512, lambda j=j, i=i: [mm(L[i][:], D["NB"], AD[:, j:j + 512], False, True)], ["L%d" % i])
            v("L%d V%s.%d" % (i, x, c), "Z%s.%d" % (x, c), 512, lambda j=j, i=i: sc(Z[:, 2048 * b + j:2048 * b + j + 512], L[i][:], Vb[:, 16 + j:528 + j], 0.0, A.min, A.max), ["L%d" % i])
        p("IB BIASC P4 DEAD%s DE%sa" % (x, x), w_ + ".0", 256, lambda: [mm(wb[0], D["IB"], D["BIASC"], True, False), mm(wb[0], D["P4"], D["DEAD" + x], False, False)], [w_])
        p(" ".join("AD%s.%d" % (x, c) for c in range(4)) + " B", w_ + ".0", 1024,
          lambda: [lanesum(wb, 0, m, AD, D["B"][:, 0:128:16], False, m == 15) for m in range(16)], [w_])
        v(w_ + ".0", "S" + x, 128, lambda: ts(D["S" + x][:, :, 0:8], wb[0], 0.0, None, A.is_gt), [w_])
        p("S%s S%s9 DEAD%s DE%sa IB NIB" % (x, x, x, x), w_ + ".1", 256, lambda: [mm(wb[1], D["IB"], D["S" + x][:, :, 1:9], True, False), mm(wb[1], D["NIB"], D["DEAD" + x], False, True)], [w_])

    def runs(t, b):
        x, y = str(b), "%d%d" % (t, b)
        wb, w_, Sx = WB[b], "W" + x, D["S" + x][:, :, 0:8]
        s("S%s K1" % x, "NS" + x, 128, lambda: act(D["NS" + x], Sx, F.Identity, bias=D["K1"], scale=-1.0))
        s("S%s K2" % x, "SP" + x, 128, lambda: act(D["SP" + x], Sx, F.Identity, bias=D["K2"]))
        v("NS%s SP%s" % (x, x), "C" + x, 64, lambda: sc(D["C" + x], D["NS" + x], D["SP" + x], 0.0, A.mult, A.add))
        s("C%s CCT" % x, "CT" + x, 128, lambda: act(D["CT" + x], D["C" + x], F.Identity, bias=D["CCT"], scale=9776.0))
        v(w_ + ".1 NK0", "CN" + x, 128, lambda: sc(D["CN" + x], D["NK0"], wb[1], 0.0, A.mult, A.add), [w_])
        s("CN" + x, "MX" + y, 16, lambda: act(D["MX" + y], D["CN" + x][:, 7::8], F.Copy))
        i = op("g", "MX" + y, "", 0.8, lambda: [send_counts(y)], sem="none")
        op("r", "", "MR" + y, 0.0, None, sem="rm" + y, inc=len(count_engines(nxt, core)), after=[i], lat=3.0)

    def upart(t, b):
        x = str(b)
        wb, w_ = WB[b], "W" + x
        zs = " ".join("Z%s.%d" % (x, c) for c in range(4))
        zo = 2048 * b
        p(zs + " P4 C129 WM", w_ + ".2", 1200, lambda: [mm(wb[2], D["P4"], D["C129"], True, False)] + [lanesum(wb, 2, m, Z[:, zo:zo + 2048], D["WM"], False, m == 15) for m in range(16)], [w_])
        p(zs + " P4 C128 WM", "UB%sa" % x, 1200, lambda: [mm(UB[b], D["P4"], D["C128"], True, False)] + [lanesum(UB, b, m, Z[:, zo:zo + 2048], D["WM"], False, False) for m in range(16)], ["UB"])
        v(w_ + ".2", "KP" + x, 128, lambda: ts(D["KP" + x], wb[2], 1.0 / 4096, -0.5 + 1.0 / 8192, A.mult, A.add), [w_])
        p("KP%s N4 UB%sa" % (x, x), "UB%s UB%sa" % (x, x), 128, lambda: [mm(UB[b], D["N4"], D["KP" + x], False, True)], ["UB"])
        s("UB%s CSQ" % x, "SQ" + x, 128, lambda: act(UB[2 + b], UB[b], F.Square, bias=D["CSQ"]), ["UB"])

    def hpart(t, b):
        x = str(b)
        v("SQ%s CT%s" % (x, x), "WI" + x, 128, lambda: tt(D["WI" + x], D["CT" + x], UB[2 + b], A.add), ["UB"])
        v("WI" + x, "HI" + x, 128, lambda: ts(D["HI" + x], D["WI" + x], 5, 4095, A.arith_shift_right, A.bitwise_and))
        v("HI" + x, "HF" + x, 128, lambda: copy(D["HF" + x], D["HI" + x]))
        p("HF%s IDF" % x, "PTH", 512, lambda: [P.transpose(PT[:, 0:128], D["HF" + x], D["IDF"])], ["PT"])
        v("PTH", "HOFF" + x, 128, lambda: copy(D["HOFF" + x], PT[:, 0:128]), ["PT"])

    def first1(t, b):
        x = str(b)
        wb, w_, FS, M0 = WB[b], "W" + x, D["FS" + x], D["MO" + x][:, 0:128]
        v("CN%s %s.1" % (x, w_), "CE" + x, 128, lambda: tt(D["CE" + x], D["CN" + x], wb[1], A.mult), [w_])
        v("CE" + x, "MO%s.0" % x, 64, lambda: ts(M0, D["CE" + x], 1.0, None, A.is_equal))
        v("MO%s.0 UB%s" % (x, x), "FS%sc" % x, 128, lambda: tt(FS[:, 128:256], M0, UB[b], A.mult), ["UB"])
        p("HF%s IDF P16 P4 KA%s " % (x, x) + " ".join("KB.%d" % k for k in range(16)), w_ + ".2", 768,
          lambda: [mm(wb[2], D["IDF"], D["HF" + x], True, False), mm(wb[2], D["P16"], D["KA" + x], False, False), mm(wb[2], D["P4"], D["KB"], False, True)], [w_])
        v("MO%s.0 %s.2" % (x, w_), "FS%sa" % x, 128, lambda: tt(FS[:, 0:128], M0, wb[2], A.mult), [w_])
        v("FR FS%sa FS%sc" % (x, x), "FO" + x, 256, lambda: sc(D["FO" + x], D["FR"], FS, 0.0, A.mult, A.add))
        for q in range(4):
            r = slice(32 * q, 32 * q + 32)
            gg("FVM FO" + x, "FV%s%d" % (x, q), 0.24, lambda r=r, q=q: gcopy(D["FVM"][r, 4 * b + q::8], D["FO" + x][r, 7::8], 32))

    def first2(t):
        p(" ".join("FV%d%d" % (b, q) for b in (0, 1) for q in range(4)) + " ".join(" PR%d" % q for q in range(4)) + " P4 ONES", "PTL", 640,
          lambda: [mm(PT[:, 256:288], D["FVM"][:, 0:128], D["PR32"], True, True), mm(PT[:, 288:320], D["P4"], D["ONES"][:, 0:32], True, False),
                   mm(PT[:, 288:320], D["FVM"][:, 128:256], D["PR32"], False, True)], ["PT"])
        LI, LQ = D["LI"], D["LQ"]
        v("PTL", "LI", 64, lambda: copy(LI, PT[:, 256:320]), ["PT"])
        v("LI", "L7", 64, lambda: ts(D["L7"], LI[:, 32:64], 4096 + 7, None, A.bitwise_and))
        v("LI", "LQa", 64, lambda: ts(LQ[:, 0:32], LI[:, 0:32], 4095, None, A.bitwise_and))
        v("LI", "LQb", 64, lambda: ts(LQ[:, 32:64], LI[:, 0:32], 12, None, A.arith_shift_right))
        v("L7 BW0", "LQc", 64, lambda: tt(LQ[:, 64:96], D["L7"], D["BW0"], A.add))
        v("LQa LQb LQc", "LOFF", 96, lambda: copy(D["LOFF"], LQ))

    def update(t):
        zs = " ".join("Z%d.%d" % (b, c) for b in (0, 1) for c in range(4))
        s(zs + " LOFF KZ", "ZS", 512 * 1.5, lambda: act(D["ZS"], Z[:].indirect(D["LOFF"][:, 32:64]), F.Identity, bias=D["KZ"]))
        v("X LOFF ZS", "ZX", 512 * 1.5, lambda: tt(D["ZX"], X[:, 0:W].indirect(D["LOFF"][:, 0:32]), D["ZS"], A.add))
        v("ZX", "ZI", 256, lambda: ts(D["ZI"], D["ZX"], 0.5, -129.0, A.mult, A.add))
        v("ZI LOFF", "X", 512 * 3.5, lambda: copy(X[:].indirect(D["LOFF"][:, 64:96]), D["ZI"]))

    def phase2(t, b):
        x = str(b)
        XH, AE = D["XH" + x], D["AE" + x]
        gather(XH, 0, D["HOFF" + x], "X HOFF" + x, "XH" + x, CALLS2[b])
        for c in range(4):
            j = 512 * c
            i = lane()
            p("Z%s.%d NIB" % (x, c), "L%d" % i, 512, lambda j=j, i=i: [mm(L[i][:], D["NIB"], Z[:, 2048 * b + j:2048 * b + j + 512], True, False)], ["L%d" % i])
            p("XH%s.%d IB" % (x, c), "L%d" % i, 512, lambda j=j, i=i: [mm(L[i][:], D["IB"], XH[:, j:j + 512], False, True)], ["L%d" % i])
            s("L%d" % i, "AE%s.%d" % (x, c), 512, lambda j=j, i=i: act(AE[:, j:j + 512], L[i][:], F.Abs), ["L%d" % i])

    def dpart(t, b):
        x = str(b)
        p(" ".join("AE%s.%d" % (x, c) for c in range(4)) + " B", "W%s.0" % x, 1024, lambda: [lanesum(WB[b], 0, m, D["AE" + x], D["B"][:, 0:128:16], True, True) for m in range(16)], ["W" + x])

    def names1(t, b):
        x, y = str(b), "%d%d" % (t, b)
        wb, w_, MO, MV = WB[b], "W" + x, D["MO" + x], D["MV" + x]
        v("S%s NM%s NM%sa" % (x, x, x), "SN" + x, 256, lambda: tt(D["SN" + x], D["S" + x][:, :, 0:8], D["NM" + x], A.mult))
        v("NS%s SN%s" % (x, x), "AX" + x, 128, lambda: sc(D["AX" + x], D["NS" + x], D["SN" + x], 0.0, A.mult, A.add))
        v("AX%s C%s" % (x, x), "T0" + x, 256, lambda: tt(D["T0" + x], D["C" + x], D["AX" + x], A.mult))
        v("T0%s A4" % x, "TI" + x, 128, lambda: ts(D["TI" + x], D["T0" + x], D["A4"], 1024.0, A.add, A.mult))
        v("TI" + x, "TJ" + x, 128, lambda: ts(D["TJ" + x], D["TI" + x], 4095 << 12, None, A.bitwise_and))
        v("TJ" + x, "P1" + x, 128, lambda: ts(PV[:, 1 + b], D["TJ" + x], 1.0, None, A.add), ["PV"])
        v("CE" + x, "CX" + x, 64, lambda: ts(D["CX" + x], D["CE" + x][:, :, 4:8], 4.5, None, A.max))
        p("CX%s MR%s IB" % (x, y), w_ + ".3", 320, lambda: [mm(wb[3][:, 0:64], D["IB"], D["CX" + x], True, False)] + [mm(wb[3][:, k:64:4], D["IB"], D["MR" + y], False, k == 3) for k in range(4)], [w_])
        for q in range(1, 4):
            v("CE" + x, "MO%s.%d" % (x, q), 64, lambda q=q: ts(MO[:, 128 * q:128 * q + 128], D["CE" + x], q + 1.0, None, A.is_equal))
        for q in range(4):
            v(w_ + ".3", "MV%s.%d" % (x, q), 64, lambda q=q: ts(MV[:, 64 * q:64 * q + 64], wb[3][:, 0:64], q + 5.0, None, A.is_equal), [w_])

    def names2(t, b):
        x, y = str(b), "%d%d" % (t, b)
        wb, w_, PRO, PRV = WB[b], "W" + x, D["PRO" + x], D["PRV" + x]
        v(w_ + ".0 C" + x, "PV.0", 128, lambda: tt(PV[:, 0], D["C" + x], wb[0], A.mult), [w_, "PV"])
        v("PV.0 HI" + x, "N2" + x, 128, lambda: tt(D["N2" + x], D["HI" + x], PV[:, 0], A.add), ["PV"])
        v("N2" + x, "N3" + x, 128, lambda: ts(D["N3" + x], D["N2" + x], 4095, None, A.bitwise_and))
        v("N3%s P1%s" % (x, x), "PV.3", 128, lambda: tt(PV[:, 3], D["N3" + x], PV[:, 1 + b], A.add), ["PV"])
        for q in range(4):
            v("MV%s.%d PV.3" % (x, q), "PRV%s.%d" % (x, q), 64, lambda q=q: tt(PRV[:, 64 * q:64 * q + 64], D["MV" + x][:, 64 * q:64 * q + 64], PV[:, 3, :, 4:8], A.mult), ["PV"])
        v(" ".join("PRV%s.%d" % (x, q) for q in range(4)) + " CRV", "OSV" + x, 256, lambda: sc(D["OSV" + x], D["CRV"], PRV, 0.0, A.mult, A.add))
        for q in range(4):
            if b:
                s("OSV" + x, "SV%s.%d" % (y, q), 64, lambda q=q: act(D["SV" + y][:, :, q], D["OSV" + x][:, 64 * q + 3:64 * q + 64:4], F.Copy))
                continue
            gg("OSV" + x, "SV%s.%d" % (y, q), 0.21, lambda q=q: gcopy(D["SV" + y][:, :, q], D["OSV" + x][:, 64 * q + 3:64 * q + 64:4], 16))
        sv = " ".join("SV%s.%d" % (y, q) for q in range(4))
        for k in (0, 2):
            for q in (k, k + 1):
                v("MO%s.%d PV.3" % (x, q), "PRO%s.%d" % (x, q), 128, lambda q=q: tt(PRO[:, 128 * q:128 * q + 128], D["MO" + x][:, 128 * q:128 * q + 128], PV[:, 3], A.mult), ["PV"])
            r = slice(128 * k, 128 * k + 256)
            v("PRO%s.%d PRO%s.%d CRO" % (x, k, x, k + 1), "OSO%s.%d" % (x, k), 256, lambda r=r: sc(D["OSO" + x][:, r], D["CRO"][:, r], PRO[:, r], 0.0, A.mult, A.add))
            for q in (k, k + 1):
                s("KM OSO%s.%d" % (x, k), "SO%s.%d" % (y, q), 64, lambda q=q: act(D["SO" + y][:, :, q], D["OSO" + x][:, 128 * q + 7:128 * q + 128:8], F.Identity, bias=D["KM"]))
        so = " ".join("SO%s.%d" % (y, q) for q in range(4))
        if t < NV - 1:
            i = op("g", so + " " + sv, "", 0.8, lambda: [send_pairs(y)], sem="none")
            op("r", "", "RO%s RV%s" % (y, y), 0.0, None, sem="rx" + y, inc=len(pair_engines(prv, core, 0)) + len(pair_engines(pr2, prv, 1)), after=[i], lat=3.5)
        else:
            i = op("g", sv, "", 0.8, lambda: [send_last(y)], sem="none")
            op("r", "", "RV" + y, 0.0, None, sem="rx" + y, inc=len(count_engines(prv, core)), after=[i], lat=3.5)

    def join(t, b):
        x, y, last = str(b), "%d%d" % (t, b), t == NV - 1
        J, NM, DE = D["J" + x], D["NM" + x], D["DEAD" + x]
        own, ov = D[("SO" if last else "RO") + y], D["RV" + y]
        rd = "RV%s " % y + (" ".join("SO%s.%d" % (y, q) for q in range(4)) if last else "RO" + y)
        if last:
            v(rd, "J" + x, 128, lambda: tt(J, own, ov, A.add))
            jt = "J" + x
        else:
            v(rd, "J%sa" % x, 112, lambda: tt(J[:, 2:16, :], own[:, 0:14, :], ov[:, 0:14, :], A.add))
            v(rd, "J%sb" % x, 64, lambda: tt(J[:, 0:2, :], own[:, 14:16, :], ov[:, 14:16, :], A.add))
            jt = "J%sa J%sb" % (x, x)
        jm, jn = J, jt
        if last:
            jm, jn = D["JM" + x], "JM" + x
            v(jt, jn, 64, lambda: ts(jm, J, 0.0, None, A.max))
        v(jn, "NM%sa" % x, 64, lambda: ts(NM[:, :, 0::2], jm, 12, None, A.arith_shift_right))
        v(jn, "NM" + x, 64, lambda: ts(NM[:, :, 1::2], jm, 4095, None, A.bitwise_and))
        v("NM%s NM%sa" % (x, x), "NF" + x, 128, lambda: copy(D["NF" + x], NM))
        p("NF%s IDF" % x, "PTN", 512, lambda: [P.transpose(PT[:, 128:256], D["NF" + x], D["IDF"])], ["PT"])
        if not last:
            v("PTN", "OFF" + x, 128, lambda: copy(D["OFF" + x], PT[:, 128:256]), ["PT"])
            v(jt, "DE%sa" % x, 64, lambda: ts(DE[:, :, 0::2], J, 0.0, None, A.is_lt))
            v(jt, "DEAD" + x, 64, lambda: ts(DE[:, :, 1::2], J, 0.0, None, A.is_lt))
        else:
            s("PTN", "YL" + x, 128, lambda: act(D["YL" + x], PT[:, 128:256], F.Copy), ["PT"])
            ld("y", "yl" + x, T.yl[:, 128 * b:128 * b + 128], D["YL" + x], "YL" + x, "yl" + x, 2.5)
            v(jt, "NA" + x, 64, lambda: ts(D["NA" + x], J, 0.0, 2.0, A.is_ge, A.mult))
            v("NA" + x, "NC" + x, 64, lambda: tt(D["NC" + x], D["NA" + x][:, :, 0:2], D["NA" + x][:, :, 2:4], A.add))
            v("NC" + x, "NN" + x, 64, lambda: tt(D["NN" + x], D["NC" + x][:, :, 0], D["NC" + x][:, :, 1], A.add))
            p("NN%s IDF" % x, "LN" + x, 1024, lambda: [P.transpose(L[0][0:8, 256 * b + w1:256 * b + 256:2], D["NN" + x][:, w1::2], D["IDF"]) for w1 in (0, 1)], ["L0"])

    def total(t):
        p("ONES MX%d0 MX%d1" % (t, t), "PTA", 128, lambda: [mm(PT[:, 288:304], D["ONES"], D["MX%d0" % t], True, False), mm(PT[:, 288:304], D["ONES"], D["MX%d1" % t], False, True)], ["PT"])
        v("PTA", "AR", 64, lambda: V.tensor_reduce(D["AR"], PT[:, 288:304], AxisListType.X, A.add), ["PT"])
        v("AR", "AI", 64, lambda: copy(D["AI"], D["AR"]))
        v("AI", "AI2", 64, lambda: ts(D["AI2"], D["AI"], 255, None, A.bitwise_and))
        v("AI2", "A4", 64, lambda: ts(D["A4"], D["AI2"], 4.0, None, A.mult))

    def count_engines(a, c):
        return topo.engines(a, c)[0:8]

    def pair_engines(a, c, k):
        e = topo.engines(a, c)
        return (e[8:16], e[0:8])[k] if len(e) == 16 else (e[0:4], e[4:8])[k]

    def mask(es):
        return sum(1 << e for e in es)
    lsum = [0]

    def send_one(dst, out, in_, sem):
        es = count_engines(core, dst)
        rid, pid, _ = topo.addr(dst)
        lsum[0] += len(es)
        g.remote_dma(D[out], D[in_], T.sem[sem], T.sem.ls, pid, rid, mask(es))

    def send_counts(y):
        send_one(prv, "MR" + y, "MX" + y, "rm" + y)

    def send_last(y):
        send_one(nxt, "RV" + y, "SV" + y, "rx" + y)

    def send_pairs(y):
        tr = []
        for k, dst, o, i in ((0, nxt, "RO", "SO"), (1, nx2, "RV", "SV")):
            es = pair_engines(core, nxt, k)
            lsum[0] += len(es)
            rid, pid, _ = topo.addr(dst)
            tr.append(RemoteDMATransfer(dst_ids=[DstId(rid=rid, pnc=pid)], dma_engine_mask=mask(es), remote_sem=T.sem["rx" + y], srcs=[D[i + y]], dsts=[D[o + y]]))
        g.remote_dma_fused(tr, local_sem=T.sem.ls)

    def part(key, fn, *a):
        cur[0] = key + "".join(str(k) for k in a[1:])
        fn(*a)
        cur[0] = ""

    for t in range(NV):
        for b in (0, 1):
            part("phase1", phase1, t, b)
            part("runs", runs, t, b)
            part("upart", upart, t, b)
            part("hpart", hpart, t, b)
        if t == 0:
            late_constants()
        for b in (0, 1):
            part("phase2", phase2, t, b)
            part("first1", first1, t, b)
            part("names1", names1, t, b)
        part("first2", first2, t)
        part("update", update, t)
        if t == NV - 1:
            ld("y", "yx", T.yx[:], X[:, 0:W], "X", "yx", 7.0)
        for b in (0, 1):
            part("dpart", dpart, t, b)
            part("names2", names2, t, b)
        if t < NV - 1:
            total(t)
        for b in (0, 1):
            part("join", join, t, b)
    v("LN0 LN1", "YN", 512, lambda: copy(D["YN"], L[0][0:8, :]), ["L0"])
    ld("y", "yn", T.yn[:], D["YN"], "YN", "yn", 2.5)
    emit(g, T, ops)
    g.wait_ge(T.sem.ls, lsum[0])


BOOST = {"runs1s": 258, "first2v": 246, "phase21p": -108, "names11v": -14, "phase10v": 32, "phase21s": -140, "upart1s": 138, "first11v": -82,
         "first10v": -16, "runs0s": 196, "phase20p": -122, "first10p": -102, "phase11p": -84}


def emit(g, T, ops):
    deps = links(ops)
    issue(g, T, ops, deps, arrange(ops, deps, BOOST, HOP)[0])


def links(ops):
    N = len(ops)
    lastw, readers, banks = {}, {}, {}
    deps = [dict() for _ in range(N)]

    def add(i, j, hard):
        if j != i:
            deps[i][j] = deps[i].get(j, False) or hard
    for i, o in enumerate(ops):
        for k in o["r"]:
            if k in lastw:
                add(i, lastw[k], True)
            readers.setdefault(k, []).append(i)
        for k in o["w"]:
            if k in lastw:
                add(i, lastw[k], not (o["q"] == "p" and ops[lastw[k]]["q"] == "p"))
            for j in readers.get(k, []):
                add(i, j, True)
            lastw[k] = i
            readers[k] = []
        for k in o["b"]:
            for j in banks.get(k, []):
                add(i, j, ops[j]["q"] != o["q"])
            banks.setdefault(k, []).append(i)
        for j in o["after"]:
            add(i, j, False)
    return deps


def arrange(ops, deps, boost, hop):
    N = len(ops)
    succ = [[] for _ in range(N)]
    for i in range(N):
        for j in deps[i]:
            succ[j].append(i)
    prio = [0.0] * N
    for i in range(N - 1, -1, -1):
        o = ops[i]
        prio[i] = o["cost"] + o["lat"] + max([prio[j] + hop for j in succ[i]] or [0.0])
    prio = [prio[i] + boost.get(ops[i]["k"], 0.0) for i in range(N)]
    left = [len(deps[i]) for i in range(N)]
    ready = [0.0] * N
    free, cand, order = {}, {}, []
    for i in range(N):
        if left[i] == 0:
            cand.setdefault(ops[i]["q"], []).append(i)
    while len(order) < N:
        best = None
        for q in sorted(cand):
            if cand[q]:
                st = max(free.get(q, 0.0), min(ready[i] for i in cand[q]))
                if best is None or st < best[0]:
                    best = (st, q)
        st, q = best
        i = max((i for i in cand[q] if ready[i] <= st + 1e-9), key=lambda i: (prio[i], -i))
        cand[q].remove(i)
        order.append(i)
        end = st + ops[i]["cost"]
        if q != "r":
            free[q] = end
        end += ops[i]["lat"]
        for j in succ[i]:
            ready[j] = max(ready[j], end + (hop if deps[j][i] and q != "r" else 0.0))
            left[j] -= 1
            if left[j] == 0:
                cand.setdefault(ops[j]["q"], []).append(j)
    return order, max(free.values())


def issue(g, T, ops, deps, order):
    queues = {"v": g.vector, "s": g.scalar, "d": g.scalar, "p": g.tensor, "g": g, "y": g.sync}
    sems = {"v": "qv", "s": "qs", "p": "qp", "g": "qg"}
    level, done, seen = {}, {}, {}
    for i in order:
        o = ops[i]
        q = o["q"]
        if q == "r":
            level[o["sem"]] = level.get(o["sem"], 0) + o["inc"]
            done[i] = (o["sem"], level[o["sem"]])
            continue
        qk = "s" if q == "d" else q
        need = {}
        for j, hard in deps[i].items():
            if hard and done[j] is not None:
                sm, c = done[j]
                need[sm] = max(need.get(sm, 0), c)
        for sm in sorted(need):
            if seen.get((qk, sm), 0) < need[sm]:
                seen[(qk, sm)] = need[sm]
                queues[q].wait_ge(T.sem[sm], need[sm])
        res = o["fn"]()
        if o["sem"] == "none":
            done[i] = None
            continue
        sm, inc = (o["sem"], o["inc"]) if o["sem"] else (sems[q], 1)
        for r in res:
            r.then_inc(T.sem[sm], inc)
            level[sm] = level.get(sm, 0) + inc
        done[i] = (sm, level[sm])
    for sm in sorted(level):
        if seen.get(("g", sm), 0) < level[sm]:
            g.wait_ge(T.sem[sm], level[sm])
